import numpy as np
import ml_dtypes


def mxq(x, axis, fmt="e4m3"):
    dtype, down = {"e4m3": (ml_dtypes.float8_e4m3fn, 7), "e5m2": (ml_dtypes.float8_e5m2, 14)}[fmt]
    v = np.moveaxis(np.asarray(x, np.float32).astype(ml_dtypes.bfloat16).astype(np.float64), axis, -1)
    blocks = v.reshape(v.shape[:-1] + (-1, 32))
    amax = np.abs(blocks).max(-1, keepdims=True)
    byte = np.maximum(np.where(amax > 0, np.frexp(amax)[1] - 1 + 127, 0) - down, 1)
    scale = np.exp2(byte - 127.0)
    codes = (blocks / scale).astype(np.float32).astype(dtype).astype(np.float64)
    return np.moveaxis((codes * scale).reshape(v.shape), -1, axis)


WIDE = False


def mx_kscale(k):
    if not WIDE:
        return np.ones(k)
    levels = np.array([10, -10, 5, -5, 0])
    if k % 512:
        return np.exp2(np.random.permutation(np.resize(levels, k // 32))).repeat(32)
    a = np.empty((k // 512, 16))
    for p in range(k // 512):
        a[p, :8] = np.random.permutation(np.resize(levels, 8))
        for g in range(8):
            far = levels[np.abs(levels - a[p, g]) >= 10]
            a[p, g + 8] = far[np.random.randint(len(far))]
    return np.exp2(a.ravel()).repeat(32)


def f64(x):
    return np.asarray(x).astype(np.float64)


def striped(idx):
    return np.tile(idx.reshape(-1, 16).T, (8, 1)).astype(np.uint16)


def unstriped(offs):
    return offs[:16].T.reshape(-1).astype(np.int64)


E2M1 = np.array([0.0, 0.5, 1.0, 1.5, 2.0, 3.0, 4.0, 6.0, -0.0, -0.5, -1.0, -1.5, -2.0, -3.0, -4.0, -6.0])


def pack_weight(w, fmt):
    k, n = w.shape
    w = f64(np.asarray(w, np.float32).astype(ml_dtypes.bfloat16)).reshape(k // 32, 32, n)
    amax = np.abs(w).max(1)
    if fmt == "e4m3":
        byte = np.frexp(amax)[1] - 1 + 127 - 7
    else:
        mant, ex = np.frexp(amax / 6.0)
        byte = np.where(mant > 0.5, ex, ex - 1) + 127
    byte = np.clip(np.where(amax > 0, byte, 1), 1, 254)
    scaled = (w * np.exp2(127.0 - byte)[:, None, :]).reshape(k, n).astype(np.float32)
    by_word = np.ascontiguousarray(scaled.reshape(k // 512, 128, 4, n).transpose(0, 1, 3, 2))
    if fmt == "e4m3":
        words = by_word.astype(ml_dtypes.float8_e4m3fn).view(np.uint8)
    else:
        c = by_word.astype(ml_dtypes.float4_e2m1fn).view(np.uint8) & 0xF
        words = (c[..., 0::2] | (c[..., 1::2] << 4)).reshape(k // 512, 128, 2 * n)
    return np.ascontiguousarray(words), np.ascontiguousarray(byte.astype(np.uint8).reshape(k // 512, 16, n))


def unpack_weight(words, scales, fmt):
    g, _, n = scales.shape
    words = np.ascontiguousarray(words).reshape(g, 128, n, -1)
    if fmt == "e4m3":
        vals = words.view(ml_dtypes.float8_e4m3fn).astype(np.float64)
    else:
        nib = np.empty((g, 128, n, 4), np.uint8)
        nib[..., 0::2] = words & 0xF
        nib[..., 1::2] = words >> 4
        vals = E2M1[nib]
    vals = vals * np.repeat(np.exp2(scales.astype(np.float64) - 127.0), 8, axis=1)[..., None]
    return vals.transpose(0, 1, 3, 2).reshape(g * 512, n)


def gelu(v):
    return 0.5 * v * (1.0 + np.tanh(np.sqrt(2.0 / np.pi) * (v + 0.044715 * v**3)))


def striped8(idx):
    return np.concatenate([v.reshape(-1, 16).T for v in idx]).astype(np.uint16)


def unstriped8(offs):
    return np.stack([offs[16 * g:16 * g + 16].T.reshape(-1) for g in range(8)]).astype(np.int64)


def runs(v, idx8):
    k = np.arange(v.shape[0])
    return v[k[:, None], idx8[k % 512 // 64]]


S, T, T2, K, K2, H, N = 1024, 2048, 2048, 1024, 512, 1024, 512

def setup_inputs():
    n = np.random.standard_normal
    s = mx_kscale(K)[:, None]
    s2 = mx_kscale(K2)[:, None]
    u = mx_kscale(H)[:, None]
    tab_words, tab_scales = pack_weight(n((K, T)) * s, "e4m3")
    tab2_words, tab2_scales = pack_weight(n((K2, T)) * s2, "e4m3")
    w2_words, w2_scales = pack_weight(0.5 * n((K2, H)) / np.sqrt(K2) / s2, "e2m1")
    return {
        "tab_words": tab_words, "tab_scales": tab_scales,
        "offs": striped8(np.stack([np.random.permutation(T)[:S] for _ in range(8)])),
        "tab2_words": tab2_words, "tab2_scales": tab2_scales,
        "offs2": striped(np.random.permutation(T)[:S]),
        "offs3": striped(np.random.permutation(T2)[:S]),
        "w1": (0.5 * n((K, H)) / np.sqrt(K) / s).astype(np.float32),
        "w2_words": w2_words, "w2_scales": w2_scales,
        "amp": (4.0 * np.exp(0.3 * n(H)) * u[:, 0]).astype(np.float32),
        "style": (0.6 * n((H, S)) * u).astype(np.float32),
        "w3": (n((H, N)) / np.sqrt(H) / u).astype(np.float32),
        "wgo": np.exp(0.3 * n((128, S))).astype(np.float32),
        "page1": n((N, T2)).astype(np.float32),
    }

def reference(tab_words, tab_scales, offs, tab2_words, tab2_scales, offs2, offs3, w1, w2_words, w2_scales, amp, style, w3, wgo, page1):
    v = runs(unpack_weight(tab_words, tab_scales, "e4m3"), unstriped8(offs))
    v2 = unpack_weight(tab2_words, tab2_scales, "e4m3")[:, unstriped(offs2)]
    w2 = unpack_weight(w2_words, w2_scales, "e2m1")
    motif = mxq(f64(w1), 0, "e4m3").T @ v
    ground = w2.T @ v2
    z = np.sin(motif) * np.sin(ground) * f64(amp)[:, None] + f64(style)
    y = mxq(f64(w3), 0, "e4m3").T @ mxq(z, 0, "e4m3")
    out = f64(page1).copy()
    out[:, unstriped(offs3)] = np.tile(f64(wgo), (N // 128, 1)) * y
    return out

@@ -1,0 +1,322 @@
+import math
+from contextlib import ExitStack
+
+import concourse.mybir as mybir
+
+S, T, K, K2, H, N = 1024, 2048, 1024, 512, 1024, 512
+FLOPS = 2 * S * (K * H + K2 * H + H * N)
+
+F32 = mybir.dt.float32
+BF16 = mybir.dt.bfloat16
+I32 = mybir.dt.int32
+U32 = mybir.dt.uint32
+U16 = mybir.dt.uint16
+U8 = mybir.dt.uint8
+FP8X4 = mybir.dt.float8_e4m3fn_x4
+FP4X4 = mybir.dt.float4_e2m1fn_x4
+MULT = mybir.AluOpType.mult
+ADD = mybir.AluOpType.add
+COPY = mybir.ActivationFunctionType.Copy
+SIN = mybir.ActivationFunctionType.Sin
+
+P = 128
+PACK = 4
+PASS = P * PACK
+CHUNK = 256
+CHUNKS = S // CHUNK
+LIST_COLS = CHUNK // 16
+TILES = CHUNKS * H // P
+LAG = 2
+RING = 5
+PHASE_BANKS = 6
+TWO_PI = 2.0 * math.pi
+ROUNDER = 1.5 * 2.0**23
+
+
+def tile_list_wallpaper_repeat_assessor_kernel(
+    tc, tab_words, tab_scales, offs, tab2_words, tab2_scales, offs2, offs3, w1, w2_words, w2_scales, amp, style, w3, wgo, page1, out
+):
+    nc = tc.nc
+    with ExitStack() as ctx:
+        held = ctx.enter_context(tc.tile_pool(name="held", bufs=1))
+        stage = ctx.enter_context(tc.tile_pool(name="stage", bufs=1))
+        work = ctx.enter_context(tc.tile_pool(name="work", bufs=1))
+        psum = ctx.enter_context(tc.psum_pool(name="psum", bufs=1))
+
+        def keep(name, shape, dtype):
+            return held.tile(shape, dtype, name=name, align_bytes=64)
+
+        motif_list = held.tile([P, S // 16], U16, name="motif_list")
+        ground_list = held.tile([P, S // 16], U16, name="ground_list")
+        page_list = held.tile([P, S // 16], U16, name="page_list")
+        nc.sync.dma_start(motif_list[:], offs)
+        nc.sync.dma_start(ground_list[:], offs2)
+
+        motif_scale_table = keep("motif_scale_table", [P, T], U8)
+        nc.vector.memset(motif_scale_table[:].bitcast(I32), 0)
+        for a in range(K // PASS):
+            for i in range(2):
+                nc.scalar.dma_start(
+                    motif_scale_table[4 * a + i : P : 16, :].bitcast(I32), tab_scales[a, i:16:2, :].bitcast(I32)
+                )
+        ground_scale_table = keep("ground_scale_table", [P, T], U8)
+        nc.vector.memset(ground_scale_table[:].bitcast(I32), 0)
+        for d in range(4):
+            nc.scalar.dma_start(
+                ground_scale_table[32 * d : 32 * d + 4, :].bitcast(I32), tab2_scales[0, 4 * d : 4 * d + 4, :].bitcast(I32)
+            )
+        w2_scale_raw = keep("w2_scale_raw", [P, H], U8)
+        nc.gpsimd.memset(w2_scale_raw[:].bitcast(I32), 0)
+        for d in range(4):
+            nc.gpsimd.dma_start(
+                w2_scale_raw[32 * d : 32 * d + 4, :].bitcast(I32), w2_scales[0, 4 * d : 4 * d + 4, :].bitcast(I32)
+            )
+        amp_cols = keep("amp_cols", [P, H // PASS, PACK], F32)
+
+        def load_rows(rows, name):
+            raw = stage.tile([P, PACK, PASS], F32, name=name, tag="weight_raw", bufs=4)
+            nc.sync.dma_start(raw[:], rows.rearrange("(p j) c -> p j c", j=PACK))
+            return raw
+
+        def load_words(words, name):
+            table = keep(name, [P, T], I32)
+            nc.sync.dma_start(table[:], words.rearrange("p t i -> p (t i)").bitcast(I32))
+            return table
+
+        def load_style(q, b):
+            rows = stage.tile([P, PACK, CHUNK], F32, name="style_rows", tag="style_rows", bufs=8)
+            nc.sync.dma_start(
+                rows[:], style[b * PASS : (b + 1) * PASS, q * CHUNK : (q + 1) * CHUNK].rearrange("(p t) j -> p t j", t=PACK)
+            )
+            return rows
+
+        def w1_block(a, b):
+            return w1[a * PASS : (a + 1) * PASS, b * PASS : (b + 1) * PASS]
+
+        w1_raw = {}
+        style_rows = {}
+        w1_raw[0, 0] = load_rows(w1_block(0, 0), "w1_raw")
+        ground_table = load_words(tab2_words[0], "ground_table")
+        w2_raw = keep("w2_raw", [P, 2 * H], U8)
+        nc.sync.dma_start(w2_raw[:].bitcast(I32), w2_words[0].bitcast(I32))
+        w1_raw[1, 0] = load_rows(w1_block(1, 0), "w1_raw")
+        motif_tables = [load_words(tab_words[a], "motif_table%d" % a) for a in range(K // PASS)]
+        nc.sync.dma_start(amp_cols[:], amp.rearrange("(b p t) -> p b t", p=P, t=PACK))
+        w1_raw[0, 1] = load_rows(w1_block(0, 1), "w1_raw")
+        style_rows[0, 0] = load_style(0, 0)
+        w1_raw[1, 1] = load_rows(w1_block(1, 1), "w1_raw")
+        style_rows[0, 1] = load_style(0, 1)
+
+        def quantise(grouped, name):
+            width = grouped.shape[1] // PACK
+            codes = keep(name + "_codes", [P, width], U32)
+            scales = keep(name + "_scales", [P, width], U8)
+            nc.vector.quantize_mx(out=codes[:].bitcast(FP8X4), scales=scales[:], in_=grouped[:])
+            return codes, scales
+
+        def quantise_w1(a, b):
+            grouped = stage.tile([P, PACK * PASS], BF16, name="grouped", tag="grouped", bufs=2, align_bytes=64)
+            nc.scalar.copy(
+                grouped[:].rearrange("p (t m j) -> p m t j", t=PACK, j=PACK),
+                w1_raw[a, b][:].rearrange("p j (m t) -> p m t j", t=PACK),
+            )
+            return quantise(grouped, "w1_%d%d" % (a, b))
+
+        def quantise_w3(raw, b):
+            grouped = stage.tile([P, PACK * PASS], BF16, name="grouped", tag="grouped", bufs=2, align_bytes=64)
+            nc.vector.tensor_copy(
+                grouped[:].rearrange("p (c i j) -> p c j i", i=4, j=PACK),
+                raw[:].rearrange("p j (c i) -> p c j i", i=4),
+            )
+            return quantise(grouped, "w3_%d" % b)
+
+        motif_scale_picked = keep("motif_scale_picked", [P, S], U8)
+        nc.vector.tensor_copy(motif_scale_picked[:], motif_scale_table[:].indirect(motif_list[:]))
+        motif_scales = keep("motif_scales", [P, S], U8)
+        nc.vector.tensor_copy(motif_scales[:].bitcast(I32), motif_scale_picked[:].bitcast(I32))
+        for a in range(K // PASS):
+            for i in range(2):
+                nc.scalar.dma_start(
+                    motif_scales[4 * a + 2 + i : P : 32, :].bitcast(I32),
+                    motif_scale_picked[16 + 4 * a + i : P : 32, :].bitcast(I32),
+                )
+        ground_scales = keep("ground_scales", [P, S], U8)
+        nc.vector.tensor_copy(ground_scales[:], ground_scale_table[:].indirect(ground_list[:]))
+
+        w1_mx = {}
+        w1_mx[0, 0] = quantise_w1(0, 0)
+
+        ground_codes = keep("ground_codes", [P, S], U32)
+        nc.vector.tensor_copy(ground_codes[:], ground_table[:].bitcast(U32).indirect(ground_list[:]))
+
+        w2_codes = keep("w2_codes", [P, 2 * H], U8)
+        nc.vector.tensor_copy(
+            w2_codes[:].bitcast(U16).rearrange("p (b t m) -> p b t m", t=PACK, m=P),
+            w2_raw[:].bitcast(U16).rearrange("p (b m t) -> p b t m", t=PACK, m=P),
+        )
+        w2_scale = keep("w2_scale", [P, H], U8)
+        nc.gpsimd.tensor_copy(
+            w2_scale[:].rearrange("p (b t m) -> p b t m", t=PACK, m=P),
+            w2_scale_raw[:].rearrange("p (b m t) -> p b t m", t=PACK, m=P),
+        )
+        w1_mx[1, 0] = quantise_w1(1, 0)
+
+        motif0 = keep("motif0", [P, S], U32)
+        nc.vector.tensor_copy(motif0[:], motif_tables[0][:].bitcast(U32).indirect(motif_list[:]))
+        motif1_first = keep("motif1_first", [P, CHUNK], U32)
+        nc.vector.tensor_copy(motif1_first[:], motif_tables[1][:].bitcast(U32).indirect(motif_list[:, :LIST_COLS]))
+        motif1_rest = keep("motif1_rest", [P, S - CHUNK], U32)
+        nc.vector.tensor_copy(motif1_rest[:], motif_tables[1][:].bitcast(U32).indirect(motif_list[:, LIST_COLS:]))
+
+        def motif_codes(a, q):
+            if a == 0:
+                return motif0[:, q * CHUNK : (q + 1) * CHUNK]
+            if q == 0:
+                return motif1_first[:]
+            return motif1_rest[:, (q - 1) * CHUNK : q * CHUNK]
+
+        w1_mx[0, 1] = quantise_w1(0, 1)
+        w1_mx[1, 1] = quantise_w1(1, 1)
+
+        w3_raw = [load_rows(w3[b * PASS : (b + 1) * PASS, :], "w3_raw") for b in range(H // PASS)]
+        for b in range(H // PASS):
+            style_rows[1, b] = load_style(1, b)
+        gain = keep("gain", [P, S], F32)
+        nc.sync.dma_start(gain[:], wgo)
+        nc.sync.dma_start(page_list[:], offs3)
+        pages = []
+        for i in range(N // P):
+            page = keep("page%d" % i, [P, T], F32)
+            nc.sync.dma_start(page[:], page1[i * P : (i + 1) * P, :])
+            pages.append(page)
+        for q in range(2, CHUNKS):
+            for b in range(H // PASS):
+                style_rows[q, b] = load_style(q, b)
+
+        def ring(n, shape, dtype, name):
+            return work.tile(shape, dtype, name=name, tag="ring%d" % (n % RING), bufs=1)
+
+        def split(u):
+            return u // (2 * PACK), u // PACK % 2, u % PACK
+
+        def reduce_phases(u):
+            q, b, t = split(u)
+            entries = slice(q * CHUNK, (q + 1) * CHUNK)
+            cols = slice(t * P, (t + 1) * P)
+            first = b * PASS + t * P
+            phase = psum.tile([P, 2 * CHUNK], F32, name="phase", tag="phase%d" % (u % PHASE_BANKS), bufs=1)
+            nc.tensor.matmul_mx(
+                out=phase[:, :CHUNK],
+                lhsT=w2_codes[:, 2 * first : 2 * (first + P)].bitcast(FP4X4),
+                lhsT_scale=w2_scale[:, first : first + P],
+                rhs=ground_codes[:, entries].bitcast(FP8X4),
+                rhs_scale=ground_scales[:, entries],
+                start=True,
+                stop=True,
+            )
+            for a in range(K // PASS):
+                codes, scales = w1_mx[a, b]
+                nc.tensor.matmul_mx(
+                    out=phase[:, CHUNK:],
+                    lhsT=codes[:, cols].bitcast(FP8X4),
+                    lhsT_scale=scales[:, cols],
+                    rhs=motif_codes(a, q).bitcast(FP8X4),
+                    rhs_scale=motif_scales[4 * a :, entries],
+                    start=(a == 0),
+                    stop=(a == K // PASS - 1),
+                )
+            shifted = ring(u, [P, 2 * CHUNK], U32, "shifted")
+            nc.scalar.activation(shifted[:], phase[:], COPY, bias=ROUNDER, scale=1.0 / TWO_PI)
+            turns = work.tile([P, 2 * CHUNK], F32, name="turns", tag="turns", bufs=4)
+            nc.scalar.activation(turns[:], shifted[:], COPY, bias=-ROUNDER, scale=1.0)
+            reduced = work.tile([P, 2 * CHUNK], F32, name="reduced", tag="reduced", bufs=4)
+            nc.vector.scalar_tensor_tensor(reduced[:], turns[:], -TWO_PI, phase[:], MULT, ADD)
+            return reduced
+
+        def multiply_sines(u, reduced, product):
+            b, t = split(u)[1:]
+            sines = ring(u + LAG, [P, 2 * CHUNK], F32, "sines")
+            nc.scalar.activation(sines[:], reduced[:], SIN)
+            nc.vector.scalar_tensor_tensor(
+                product[:, t, :], sines[:, CHUNK:], amp_cols[:, b, t : t + 1], sines[:, :CHUNK], MULT, MULT
+            )
+
+        def quantise_z(q, b, product):
+            z = work.tile([P, CHUNK * PACK], BF16, name="z", tag="z", bufs=2, align_bytes=64)
+            nc.vector.tensor_tensor(
+                z[:].rearrange("p (c i t) -> p c t i", i=4, t=PACK),
+                product[:].rearrange("p t (c i) -> p c t i", i=4),
+                style_rows[q, b][:].rearrange("p t (c i) -> p c t i", i=4),
+                ADD,
+            )
+            codes = work.tile([P, CHUNK], U32, name="z_codes", tag="z_codes", bufs=4, align_bytes=64)
+            scales = work.tile([P, CHUNK], U8, name="z_scales", tag="z_scales", bufs=4, align_bytes=64)
+            nc.vector.quantize_mx(out=codes[:].bitcast(FP8X4), scales=scales[:], in_=z[:])
+            return codes, scales
+
+        def last_product(z_mx):
+            halves = []
+            for pair in range(N // P // 2):
+                sums = psum.tile([P, 2, CHUNK], F32, name="sums", tag="sums%d" % pair, bufs=1)
+                for half in range(2):
+                    cols = slice((2 * pair + half) * P, (2 * pair + half + 1) * P)
+                    for b in range(H // PASS):
+                        nc.tensor.matmul_mx(
+                            out=sums[:, half, :],
+                            lhsT=w3_mx[b][0][:, cols].bitcast(FP8X4),
+                            lhsT_scale=w3_mx[b][1][:, cols],
+                            rhs=z_mx[b][0][:].bitcast(FP8X4),
+                            rhs_scale=z_mx[b][1][:],
+                            start=(b == 0),
+                            stop=(b == H // PASS - 1),
+                        )
+                    halves.append(sums[:, half, :])
+            return halves
+
+        def scatter(i, first_chunk, chunks, y):
+            nc.vector.tensor_tensor(
+                pages[i][:].indirect(page_list[:, first_chunk * LIST_COLS : (first_chunk + chunks) * LIST_COLS]),
+                y,
+                gain[:, first_chunk * CHUNK : (first_chunk + chunks) * CHUNK],
+                MULT,
+            )
+
+        w3_mx = []
+        reduced = {}
+        z_mx = []
+        sums = None
+        product = None
+        y_last_page = work.tile([P, 2 * CHUNK], F32, name="y_last_page")
+        for n in range(TILES + LAG):
+            if n < TILES:
+                reduced[n] = reduce_phases(n)
+            u = n - LAG
+            if u < 0:
+                continue
+            q, b, t = split(u)
+            if t == 0:
+                product = work.tile([P, PACK, CHUNK], F32, name="product", tag="product", bufs=2)
+            multiply_sines(u, reduced[u], product)
+            if q > 0 and t % 2 == 0:
+                i = 2 * b + t // 2
+                if q == CHUNKS - 1 and i == N // P - 1:
+                    nc.scalar.copy(y_last_page[:, :CHUNK], sums[i])
+                else:
+                    y = ring(u + LAG, [P, CHUNK], F32, "y")
+                    nc.scalar.copy(y[:], sums[i])
+                    scatter(i, q - 1, 1, y[:])
+            if t == PACK - 1:
+                z_mx.append(quantise_z(q, b, product))
+                if q == 0:
+                    w3_mx.append(quantise_w3(w3_raw[b], b))
+                if b == 1:
+                    sums = last_product(z_mx)
+                    z_mx = []
+        for i in range(N // P - 1):
+            y = work.tile([P, CHUNK], F32, name="y_end", tag="y_end", bufs=3)
+            nc.scalar.copy(y[:], sums[i])
+            scatter(i, CHUNKS - 1, 1, y[:])
+        nc.scalar.copy(y_last_page[:, CHUNK:], sums[N // P - 1])
+        scatter(N // P - 1, CHUNKS - 2, 2, y_last_page[:])
+        for i in range(N // P):
+            nc.sync.dma_start(out[i * P : (i + 1) * P, :], pages[i][:])

@@ -25,9 +25,11 @@ PASS = P * PACK
 CHUNK = 256
 CHUNKS = S // CHUNK
 LIST_COLS = CHUNK // 16
-TILES = CHUNKS * H // P
 LAG = 2
-RING = 5
+RING = 9
+TURNS_RING = 10
+HALF = CHUNK // 2
+HOLD = 4
 PHASE_BANKS = 6
 TWO_PI = 2.0 * math.pi
 ROUNDER = 1.5 * 2.0**23
@@ -49,28 +51,6 @@ def tile_list_wallpaper_repeat_assessor_kernel(
         motif_list = held.tile([P, S // 16], U16, name="motif_list")
         ground_list = held.tile([P, S // 16], U16, name="ground_list")
         page_list = held.tile([P, S // 16], U16, name="page_list")
-        nc.sync.dma_start(motif_list[:], offs)
-        nc.sync.dma_start(ground_list[:], offs2)
-
-        motif_scale_table = keep("motif_scale_table", [P, T], U8)
-        nc.vector.memset(motif_scale_table[:].bitcast(I32), 0)
-        for a in range(K // PASS):
-            for i in range(2):
-                nc.scalar.dma_start(
-                    motif_scale_table[4 * a + i : P : 16, :].bitcast(I32), tab_scales[a, i:16:2, :].bitcast(I32)
-                )
-        ground_scale_table = keep("ground_scale_table", [P, T], U8)
-        nc.vector.memset(ground_scale_table[:].bitcast(I32), 0)
-        for d in range(4):
-            nc.scalar.dma_start(
-                ground_scale_table[32 * d : 32 * d + 4, :].bitcast(I32), tab2_scales[0, 4 * d : 4 * d + 4, :].bitcast(I32)
-            )
-        w2_scale_raw = keep("w2_scale_raw", [P, H], U8)
-        nc.gpsimd.memset(w2_scale_raw[:].bitcast(I32), 0)
-        for d in range(4):
-            nc.gpsimd.dma_start(
-                w2_scale_raw[32 * d : 32 * d + 4, :].bitcast(I32), w2_scales[0, 4 * d : 4 * d + 4, :].bitcast(I32)
-            )
         amp_cols = keep("amp_cols", [P, H // PASS, PACK], F32)
 
         def load_rows(rows, name):
@@ -95,10 +75,32 @@ def tile_list_wallpaper_repeat_assessor_kernel(
 
         w1_raw = {}
         style_rows = {}
+        ground_scale_table = keep("ground_scale_table", [P, T], U8)
+        nc.vector.memset(ground_scale_table[:].bitcast(I32), 0)
+        w2_scale_raw = keep("w2_scale_raw", [P, H], U8)
+        nc.vector.memset(w2_scale_raw[:].bitcast(I32), 0)
+        motif_scale_table = keep("motif_scale_table", [P, T], U8)
+        nc.vector.memset(motif_scale_table[:].bitcast(I32), 0)
+
         w1_raw[0, 0] = load_rows(w1_block(0, 0), "w1_raw")
+        nc.sync.dma_start(ground_list[:], offs2)
+        for d in range(4):
+            nc.sync.dma_start(
+                ground_scale_table[32 * d : 32 * d + 4, :].bitcast(I32), tab2_scales[0, 4 * d : 4 * d + 4, :].bitcast(I32)
+            )
         ground_table = load_words(tab2_words[0], "ground_table")
         w2_raw = keep("w2_raw", [P, 2 * H], U8)
         nc.sync.dma_start(w2_raw[:].bitcast(I32), w2_words[0].bitcast(I32))
+        for d in range(4):
+            nc.sync.dma_start(
+                w2_scale_raw[32 * d : 32 * d + 4, :].bitcast(I32), w2_scales[0, 4 * d : 4 * d + 4, :].bitcast(I32)
+            )
+        nc.sync.dma_start(motif_list[:], offs)
+        for a in range(K // PASS):
+            for i in range(2):
+                nc.sync.dma_start(
+                    motif_scale_table[4 * a + i : P : 16, :].bitcast(I32), tab_scales[a, i:16:2, :].bitcast(I32)
+                )
         w1_raw[1, 0] = load_rows(w1_block(1, 0), "w1_raw")
         motif_tables = [load_words(tab_words[a], "motif_table%d" % a) for a in range(K // PASS)]
         nc.sync.dma_start(amp_cols[:], amp.rearrange("(b p t) -> p b t", p=P, t=PACK))
@@ -115,65 +117,67 @@ def tile_list_wallpaper_repeat_assessor_kernel(
             return codes, scales
 
         def quantise_w1(a, b):
-            grouped = stage.tile([P, PACK * PASS], BF16, name="grouped", tag="grouped", bufs=2, align_bytes=64)
-            nc.scalar.copy(
-                grouped[:].rearrange("p (t m j) -> p m t j", t=PACK, j=PACK),
-                w1_raw[a, b][:].rearrange("p j (m t) -> p m t j", t=PACK),
-            )
+            grouped = stage.tile([P, PACK * PASS], BF16, name="grouped", tag="grouped", bufs=3, align_bytes=64)
+            dealt = grouped[:].rearrange("p (t m j) -> p m t j", t=PACK, j=PACK)
+            rows = w1_raw[a, b][:].rearrange("p j (m t) -> p m t j", t=PACK)
+            if b == 0:
+                nc.scalar.copy(dealt, rows)
+            else:
+                nc.gpsimd.tensor_scalar(dealt, rows, 1.0, 0.0, MULT, ADD)
             return quantise(grouped, "w1_%d%d" % (a, b))
 
         def quantise_w3(raw, b):
-            grouped = stage.tile([P, PACK * PASS], BF16, name="grouped", tag="grouped", bufs=2, align_bytes=64)
-            nc.vector.tensor_copy(
+            grouped = stage.tile([P, PACK * PASS], BF16, name="grouped", tag="grouped", bufs=3, align_bytes=64)
+            nc.scalar.copy(
                 grouped[:].rearrange("p (c i j) -> p c j i", i=4, j=PACK),
                 raw[:].rearrange("p j (c i) -> p c j i", i=4),
             )
             return quantise(grouped, "w3_%d" % b)
 
-        motif_scale_picked = keep("motif_scale_picked", [P, S], U8)
-        nc.vector.tensor_copy(motif_scale_picked[:], motif_scale_table[:].indirect(motif_list[:]))
-        motif_scales = keep("motif_scales", [P, S], U8)
-        nc.vector.tensor_copy(motif_scales[:].bitcast(I32), motif_scale_picked[:].bitcast(I32))
-        for a in range(K // PASS):
-            for i in range(2):
-                nc.scalar.dma_start(
-                    motif_scales[4 * a + 2 + i : P : 32, :].bitcast(I32),
-                    motif_scale_picked[16 + 4 * a + i : P : 32, :].bitcast(I32),
-                )
-        ground_scales = keep("ground_scales", [P, S], U8)
-        nc.vector.tensor_copy(ground_scales[:], ground_scale_table[:].indirect(ground_list[:]))
+        def gather(table, offsets, dtype, name, chunks):
+            width = (chunks.stop - chunks.start) * CHUNK
+            picked = keep(name, [P, width], dtype)
+            nc.vector.tensor_copy(picked[:], table.indirect(offsets[:, chunks.start * LIST_COLS : chunks.stop * LIST_COLS]))
+            return picked
 
-        w1_mx = {}
-        w1_mx[0, 0] = quantise_w1(0, 0)
+        def chunk_of(first, rest, q):
+            return first[:] if q == 0 else rest[:, (q - 1) * CHUNK : q * CHUNK]
 
-        ground_codes = keep("ground_codes", [P, S], U32)
-        nc.vector.tensor_copy(ground_codes[:], ground_table[:].bitcast(U32).indirect(ground_list[:]))
-
+        FIRST, REST, WHOLE = slice(0, 1), slice(1, CHUNKS), slice(0, CHUNKS)
+        ground_scales_first = gather(ground_scale_table[:], ground_list, U8, "ground_scales_first", FIRST)
+        w2_scale = keep("w2_scale", [P, H], U8)
+        nc.vector.tensor_copy(
+            w2_scale[:].rearrange("p (b t m) -> p b t m", t=PACK, m=P),
+            w2_scale_raw[:].rearrange("p (b m t) -> p b t m", t=PACK, m=P),
+        )
+        ground_first = gather(ground_table[:].bitcast(U32), ground_list, U32, "ground_first", FIRST)
         w2_codes = keep("w2_codes", [P, 2 * H], U8)
         nc.vector.tensor_copy(
             w2_codes[:].bitcast(U16).rearrange("p (b t m) -> p b t m", t=PACK, m=P),
             w2_raw[:].bitcast(U16).rearrange("p (b m t) -> p b t m", t=PACK, m=P),
         )
-        w2_scale = keep("w2_scale", [P, H], U8)
-        nc.gpsimd.tensor_copy(
-            w2_scale[:].rearrange("p (b t m) -> p b t m", t=PACK, m=P),
-            w2_scale_raw[:].rearrange("p (b m t) -> p b t m", t=PACK, m=P),
-        )
+
+        motif_scale_picked = gather(motif_scale_table[:], motif_list, U8, "motif_scale_picked", WHOLE)
+        motif_scales = keep("motif_scales", [P, S], U8)
+        nc.vector.tensor_copy(motif_scales[:].bitcast(I32), motif_scale_picked[:].bitcast(I32))
+        for a in range(K // PASS):
+            for i in range(2):
+                nc.gpsimd.dma_start(
+                    motif_scales[4 * a + 2 + i : P : 32, :].bitcast(I32),
+                    motif_scale_picked[16 + 4 * a + i : P : 32, :].bitcast(I32),
+                )
+
+        w1_mx = {}
+        w1_mx[0, 0] = quantise_w1(0, 0)
         w1_mx[1, 0] = quantise_w1(1, 0)
-
-        motif0 = keep("motif0", [P, S], U32)
-        nc.vector.tensor_copy(motif0[:], motif_tables[0][:].bitcast(U32).indirect(motif_list[:]))
-        motif1_first = keep("motif1_first", [P, CHUNK], U32)
-        nc.vector.tensor_copy(motif1_first[:], motif_tables[1][:].bitcast(U32).indirect(motif_list[:, :LIST_COLS]))
-        motif1_rest = keep("motif1_rest", [P, S - CHUNK], U32)
-        nc.vector.tensor_copy(motif1_rest[:], motif_tables[1][:].bitcast(U32).indirect(motif_list[:, LIST_COLS:]))
-
-        def motif_codes(a, q):
-            if a == 0:
-                return motif0[:, q * CHUNK : (q + 1) * CHUNK]
-            if q == 0:
-                return motif1_first[:]
-            return motif1_rest[:, (q - 1) * CHUNK : q * CHUNK]
+        motif_first = [
+            gather(motif_tables[a][:].bitcast(U32), motif_list, U32, "motif_first%d" % a, FIRST) for a in range(K // PASS)
+        ]
+        ground_scales_rest = gather(ground_scale_table[:], ground_list, U8, "ground_scales_rest", REST)
+        ground_rest = gather(ground_table[:].bitcast(U32), ground_list, U32, "ground_rest", REST)
+        motif_rest = [
+            gather(motif_tables[a][:].bitcast(U32), motif_list, U32, "motif_rest%d" % a, REST) for a in range(K // PASS)
+        ]
 
         w1_mx[0, 1] = quantise_w1(0, 1)
         w1_mx[1, 1] = quantise_w1(1, 1)
@@ -194,82 +198,83 @@ def tile_list_wallpaper_repeat_assessor_kernel(
                 style_rows[q, b] = load_style(q, b)
 
         def ring(n, shape, dtype, name):
-            return work.tile(shape, dtype, name=name, tag="ring%d" % (n % RING), bufs=1)
+            return work.tile(shape, dtype, name=name, tag="ring%d" % (n % RING), bufs=1, align_bytes=64)
 
-        def split(u):
-            return u // (2 * PACK), u // PACK % 2, u % PACK
+        def turns_ring(n, shape, dtype, name):
+            return work.tile(shape, dtype, name=name, tag="turns%d" % (n % TURNS_RING), bufs=1, align_bytes=64)
 
-        def reduce_phases(u):
-            q, b, t = split(u)
-            entries = slice(q * CHUNK, (q + 1) * CHUNK)
-            cols = slice(t * P, (t + 1) * P)
+        def ground_product(phase, q, b, t):
             first = b * PASS + t * P
-            phase = psum.tile([P, 2 * CHUNK], F32, name="phase", tag="phase%d" % (u % PHASE_BANKS), bufs=1)
             nc.tensor.matmul_mx(
-                out=phase[:, :CHUNK],
+                out=phase,
                 lhsT=w2_codes[:, 2 * first : 2 * (first + P)].bitcast(FP4X4),
                 lhsT_scale=w2_scale[:, first : first + P],
-                rhs=ground_codes[:, entries].bitcast(FP8X4),
-                rhs_scale=ground_scales[:, entries],
+                rhs=chunk_of(ground_first, ground_rest, q).bitcast(FP8X4),
+                rhs_scale=chunk_of(ground_scales_first, ground_scales_rest, q),
                 start=True,
                 stop=True,
             )
+
+        def motif_product(phase, q, b, t):
+            cols = slice(t * P, (t + 1) * P)
             for a in range(K // PASS):
                 codes, scales = w1_mx[a, b]
                 nc.tensor.matmul_mx(
-                    out=phase[:, CHUNK:],
+                    out=phase,
                     lhsT=codes[:, cols].bitcast(FP8X4),
                     lhsT_scale=scales[:, cols],
-                    rhs=motif_codes(a, q).bitcast(FP8X4),
-                    rhs_scale=motif_scales[4 * a :, entries],
+                    rhs=chunk_of(motif_first[a], motif_rest[a], q).bitcast(FP8X4),
+                    rhs_scale=motif_scales[4 * a :, q * CHUNK : (q + 1) * CHUNK],
                     start=(a == 0),
                     stop=(a == K // PASS - 1),
                 )
-            shifted = ring(u, [P, 2 * CHUNK], U32, "shifted")
+
+        def reduce_phases(n, first_product, q, b, h):
+            phase = psum.tile([P, 2, CHUNK], F32, name="phase", tag="phase%d" % (n % PHASE_BANKS), bufs=1)
+            for e in range(2):
+                first_product(phase[:, e, :], q, b, 2 * h + e)
+            shifted = ring(n, [P, 2, CHUNK], U32, "shifted")
             nc.scalar.activation(shifted[:], phase[:], COPY, bias=ROUNDER, scale=1.0 / TWO_PI)
-            turns = work.tile([P, 2 * CHUNK], F32, name="turns", tag="turns", bufs=4)
+            turns = turns_ring(n, [P, 2, CHUNK], F32, "turns")
             nc.scalar.activation(turns[:], shifted[:], COPY, bias=-ROUNDER, scale=1.0)
-            reduced = work.tile([P, 2 * CHUNK], F32, name="reduced", tag="reduced", bufs=4)
+            reduced = work.tile([P, 2, CHUNK], F32, name="reduced", tag="reduced", bufs=4)
             nc.vector.scalar_tensor_tensor(reduced[:], turns[:], -TWO_PI, phase[:], MULT, ADD)
             return reduced
 
-        def multiply_sines(u, reduced, product):
-            b, t = split(u)[1:]
-            sines = ring(u + LAG, [P, 2 * CHUNK], F32, "sines")
-            nc.scalar.activation(sines[:], reduced[:], SIN)
-            nc.vector.scalar_tensor_tensor(
-                product[:, t, :], sines[:, CHUNK:], amp_cols[:, b, t : t + 1], sines[:, :CHUNK], MULT, MULT
-            )
-
-        def quantise_z(q, b, product):
-            z = work.tile([P, CHUNK * PACK], BF16, name="z", tag="z", bufs=2, align_bytes=64)
-            nc.vector.tensor_tensor(
+        def add_style(engine, slot, q, b, e, product):
+            cols = slice(e * HALF, (e + 1) * HALF)
+            z = ring(slot, [P, HALF * PACK], BF16, "z")
+            engine.tensor_tensor(
                 z[:].rearrange("p (c i t) -> p c t i", i=4, t=PACK),
-                product[:].rearrange("p t (c i) -> p c t i", i=4),
-                style_rows[q, b][:].rearrange("p t (c i) -> p c t i", i=4),
+                product[:, :, cols].rearrange("p t (c i) -> p c t i", i=4),
+                style_rows[q, b][:, :, cols].rearrange("p t (c i) -> p c t i", i=4),
                 ADD,
             )
-            codes = work.tile([P, CHUNK], U32, name="z_codes", tag="z_codes", bufs=4, align_bytes=64)
-            scales = work.tile([P, CHUNK], U8, name="z_scales", tag="z_scales", bufs=4, align_bytes=64)
+            return z
+
+        def quantise_z(slot, z):
+            codes = turns_ring(slot, [P, HALF], U32, "z_codes")
+            scales = work.tile([P, HALF], U8, name="z_scales", tag="z_scales", bufs=8, align_bytes=64)
             nc.vector.quantize_mx(out=codes[:].bitcast(FP8X4), scales=scales[:], in_=z[:])
             return codes, scales
 
-        def last_product(z_mx):
+        def last_product(q):
             halves = []
             for pair in range(N // P // 2):
                 sums = psum.tile([P, 2, CHUNK], F32, name="sums", tag="sums%d" % pair, bufs=1)
                 for half in range(2):
                     cols = slice((2 * pair + half) * P, (2 * pair + half + 1) * P)
-                    for b in range(H // PASS):
-                        nc.tensor.matmul_mx(
-                            out=sums[:, half, :],
-                            lhsT=w3_mx[b][0][:, cols].bitcast(FP8X4),
-                            lhsT_scale=w3_mx[b][1][:, cols],
-                            rhs=z_mx[b][0][:].bitcast(FP8X4),
-                            rhs_scale=z_mx[b][1][:],
-                            start=(b == 0),
-                            stop=(b == H // PASS - 1),
-                        )
+                    for e in range(2):
+                        for b in range(H // PASS):
+                            nc.tensor.matmul_mx(
+                                out=sums[:, half, e * HALF : (e + 1) * HALF],
+                                lhsT=w3_mx[b][0][:, cols].bitcast(FP8X4),
+                                lhsT_scale=w3_mx[b][1][:, cols],
+                                rhs=z_mx[q, b, e][0][:].bitcast(FP8X4),
+                                rhs_scale=z_mx[q, b, e][1][:],
+                                start=(b == 0),
+                                stop=(b == H // PASS - 1),
+                            )
                     halves.append(sums[:, half, :])
             return halves
 
@@ -281,42 +286,76 @@ def tile_list_wallpaper_repeat_assessor_kernel(
                 MULT,
             )
 
+        pairs = [(b, h) for b in range(H // PASS) for h in range(PACK // 2)]
+        steps = [(ground_product, 0, b, h) for b, h in pairs] + [(motif_product, 0, b, h) for b, h in pairs]
+        for q in range(1, CHUNKS):
+            for b, h in pairs:
+                steps.extend([(ground_product, q, b, h), (motif_product, q, b, h)])
+
         w3_mx = []
         reduced = {}
-        z_mx = []
-        sums = None
-        product = None
-        y_last_page = work.tile([P, 2 * CHUNK], F32, name="y_last_page")
-        for n in range(TILES + LAG):
-            if n < TILES:
-                reduced[n] = reduce_phases(n)
-            u = n - LAG
-            if u < 0:
+        ground_sines = {}
+        z_mx = {}
+        sums = {}
+        products = {}
+        to_add = []
+        to_quantise = {}
+        to_place = []
+        last = len(steps) - 1
+        y_late = [work.tile([P, 2 * CHUNK], F32, name="y_late%d" % i) for i in range(2)]
+        for n in range(len(steps) + LAG):
+            if n < len(steps):
+                reduced[n] = reduce_phases(n, *steps[n])
+            if n in to_quantise:
+                key, z = to_quantise[n]
+                z_mx[key] = quantise_z(n, z)
+                if key[1:] == (1, 1):
+                    sums[key[0]] = last_product(key[0])
+                    to_place.extend([(key[0], i) for i in range(N // P)])
+            if n < LAG:
                 continue
-            q, b, t = split(u)
-            if t == 0:
-                product = work.tile([P, PACK, CHUNK], F32, name="product", tag="product", bufs=2)
-            multiply_sines(u, reduced[u], product)
-            if q > 0 and t % 2 == 0:
-                i = 2 * b + t // 2
-                if q == CHUNKS - 1 and i == N // P - 1:
-                    nc.scalar.copy(y_last_page[:, :CHUNK], sums[i])
-                else:
-                    y = ring(u + LAG, [P, CHUNK], F32, "y")
-                    nc.scalar.copy(y[:], sums[i])
-                    scatter(i, q - 1, 1, y[:])
-            if t == PACK - 1:
-                z_mx.append(quantise_z(q, b, product))
+            m = n - LAG
+            first_product, q, b, h = steps[m]
+            sines = ring(n, [P, 2, CHUNK], F32, "sines")
+            nc.scalar.activation(sines[:], reduced[m][:], SIN)
+            if first_product is ground_product:
+                ground_sines[q, b, h] = (sines, n)
+                continue
+            if h == 0:
+                products[q, b] = work.tile([P, PACK, CHUNK], F32, name="product", tag="product", bufs=2)
+            ground, ground_slot = ground_sines[q, b, h]
+            for e in range(2):
+                t = 2 * h + e
+                nc.vector.scalar_tensor_tensor(
+                    products[q, b][:, t, :], sines[:, e, :], amp_cols[:, b, t : t + 1], ground[:, e, :], MULT, MULT
+                )
+            if to_place and m < last:
+                done, i = to_place.pop(0)
+                y = ring(n, [P, CHUNK], F32, "y")
+                nc.scalar.copy(y[:], sums[done][i])
+                scatter(i, done, 1, y[:])
+            if h == 1:
+                to_add.extend([(q, b, 0), (q, b, 1)])
                 if q == 0:
                     w3_mx.append(quantise_w3(w3_raw[b], b))
-                if b == 1:
-                    sums = last_product(z_mx)
-                    z_mx = []
-        for i in range(N // P - 1):
-            y = work.tile([P, CHUNK], F32, name="y_end", tag="y_end", bufs=3)
-            nc.scalar.copy(y[:], sums[i])
+            if to_add and m < last:
+                key = to_add.pop(0)
+                z = add_style(nc.gpsimd, ground_slot, *key, products[key[:2]])
+                to_quantise[min(m + HOLD, last + LAG)] = (key, z)
+
+        end = last + LAG
+        for k in range(2):
+            nc.scalar.copy(y_late[k][:, :CHUNK], sums[CHUNKS - 2][2 + k])
+        z_end = [add_style(nc.vector, end + 1 + k, *key, products[key[:2]]) for k, key in enumerate(to_add)]
+        for k, key in enumerate(to_add):
+            z_mx[key] = quantise_z(end + 1 + k, z_end[k])
+        sums_end = last_product(CHUNKS - 1)
+        for i in range(2):
+            y = work.tile([P, CHUNK], F32, name="y_end", tag="y_end", bufs=2)
+            nc.scalar.copy(y[:], sums_end[i])
             scatter(i, CHUNKS - 1, 1, y[:])
-        nc.scalar.copy(y_last_page[:, CHUNK:], sums[N // P - 1])
-        scatter(N // P - 1, CHUNKS - 2, 2, y_last_page[:])
+        for k in range(2):
+            nc.scalar.copy(y_late[k][:, CHUNK:], sums_end[2 + k])
+            scatter(2 + k, CHUNKS - 2, 2, y_late[k][:])
         for i in range(N // P):
             nc.sync.dma_start(out[i * P : (i + 1) * P, :], pages[i][:])

@@ -75,38 +75,38 @@ def tile_list_wallpaper_repeat_assessor_kernel(
 
         w1_raw = {}
         style_rows = {}
+        motif_scale_table = keep("motif_scale_table", [P, T], U8)
+        nc.vector.memset(motif_scale_table[:].bitcast(I32), 0)
         ground_scale_table = keep("ground_scale_table", [P, T], U8)
         nc.vector.memset(ground_scale_table[:].bitcast(I32), 0)
         w2_scale_raw = keep("w2_scale_raw", [P, H], U8)
-        nc.vector.memset(w2_scale_raw[:].bitcast(I32), 0)
-        motif_scale_table = keep("motif_scale_table", [P, T], U8)
-        nc.vector.memset(motif_scale_table[:].bitcast(I32), 0)
-
-        w1_raw[0, 0] = load_rows(w1_block(0, 0), "w1_raw")
-        nc.sync.dma_start(ground_list[:], offs2)
+        nc.gpsimd.memset(w2_scale_raw[:].bitcast(I32), 0)
+        for a in range(K // PASS):
+            for i in range(2):
+                nc.scalar.dma_start(
+                    motif_scale_table[4 * a + i : P : 16, :].bitcast(I32), tab_scales[a, i:16:2, :].bitcast(I32)
+                )
         for d in range(4):
-            nc.sync.dma_start(
+            nc.scalar.dma_start(
                 ground_scale_table[32 * d : 32 * d + 4, :].bitcast(I32), tab2_scales[0, 4 * d : 4 * d + 4, :].bitcast(I32)
             )
+        for d in range(4):
+            nc.gpsimd.dma_start(
+                w2_scale_raw[32 * d : 32 * d + 4, :].bitcast(I32), w2_scales[0, 4 * d : 4 * d + 4, :].bitcast(I32)
+            )
+
+        nc.sync.dma_start(motif_list[:], offs)
+        nc.sync.dma_start(ground_list[:], offs2)
+        w1_raw[0, 0] = load_rows(w1_block(0, 0), "w1_raw")
         ground_table = load_words(tab2_words[0], "ground_table")
         w2_raw = keep("w2_raw", [P, 2 * H], U8)
         nc.sync.dma_start(w2_raw[:].bitcast(I32), w2_words[0].bitcast(I32))
-        for d in range(4):
-            nc.sync.dma_start(
-                w2_scale_raw[32 * d : 32 * d + 4, :].bitcast(I32), w2_scales[0, 4 * d : 4 * d + 4, :].bitcast(I32)
-            )
-        nc.sync.dma_start(motif_list[:], offs)
-        for a in range(K // PASS):
-            for i in range(2):
-                nc.sync.dma_start(
-                    motif_scale_table[4 * a + i : P : 16, :].bitcast(I32), tab_scales[a, i:16:2, :].bitcast(I32)
-                )
         w1_raw[1, 0] = load_rows(w1_block(1, 0), "w1_raw")
-        motif_tables = [load_words(tab_words[a], "motif_table%d" % a) for a in range(K // PASS)]
-        nc.sync.dma_start(amp_cols[:], amp.rearrange("(b p t) -> p b t", p=P, t=PACK))
         w1_raw[0, 1] = load_rows(w1_block(0, 1), "w1_raw")
-        style_rows[0, 0] = load_style(0, 0)
+        motif_tables = [load_words(tab_words[a], "motif_table%d" % a) for a in range(K // PASS)]
         w1_raw[1, 1] = load_rows(w1_block(1, 1), "w1_raw")
+        nc.sync.dma_start(amp_cols[:], amp.rearrange("(b p t) -> p b t", p=P, t=PACK))
+        style_rows[0, 0] = load_style(0, 0)
         style_rows[0, 1] = load_style(0, 1)
 
         def quantise(grouped, name):
@@ -120,15 +120,15 @@ def tile_list_wallpaper_repeat_assessor_kernel(
             grouped = stage.tile([P, PACK * PASS], BF16, name="grouped", tag="grouped", bufs=3, align_bytes=64)
             dealt = grouped[:].rearrange("p (t m j) -> p m t j", t=PACK, j=PACK)
             rows = w1_raw[a, b][:].rearrange("p j (m t) -> p m t j", t=PACK)
-            if b == 0:
-                nc.scalar.copy(dealt, rows)
+            if (a, b) != (1, 1):
+                nc.scalar.activation(dealt, rows, COPY)
             else:
                 nc.gpsimd.tensor_scalar(dealt, rows, 1.0, 0.0, MULT, ADD)
             return quantise(grouped, "w1_%d%d" % (a, b))
 
         def quantise_w3(raw, b):
             grouped = stage.tile([P, PACK * PASS], BF16, name="grouped", tag="grouped", bufs=3, align_bytes=64)
-            nc.scalar.copy(
+            nc.vector.tensor_copy(
                 grouped[:].rearrange("p (c i j) -> p c j i", i=4, j=PACK),
                 raw[:].rearrange("p j (c i) -> p c j i", i=4),
             )
@@ -144,9 +144,19 @@ def tile_list_wallpaper_repeat_assessor_kernel(
             return first[:] if q == 0 else rest[:, (q - 1) * CHUNK : q * CHUNK]
 
         FIRST, REST, WHOLE = slice(0, 1), slice(1, CHUNKS), slice(0, CHUNKS)
+        motif_scale_picked = gather(motif_scale_table[:], motif_list, U8, "motif_scale_picked", WHOLE)
+        motif_scales = keep("motif_scales", [P, S], U8)
+        nc.vector.tensor_copy(motif_scales[:].bitcast(I32), motif_scale_picked[:].bitcast(I32))
+        for a in range(K // PASS):
+            for i in range(2):
+                nc.scalar.dma_start(
+                    motif_scales[4 * a + 2 + i : P : 32, :].bitcast(I32),
+                    motif_scale_picked[16 + 4 * a + i : P : 32, :].bitcast(I32),
+                )
+
         ground_scales_first = gather(ground_scale_table[:], ground_list, U8, "ground_scales_first", FIRST)
         w2_scale = keep("w2_scale", [P, H], U8)
-        nc.vector.tensor_copy(
+        nc.gpsimd.tensor_copy(
             w2_scale[:].rearrange("p (b t m) -> p b t m", t=PACK, m=P),
             w2_scale_raw[:].rearrange("p (b m t) -> p b t m", t=PACK, m=P),
         )
@@ -157,19 +167,10 @@ def tile_list_wallpaper_repeat_assessor_kernel(
             w2_raw[:].bitcast(U16).rearrange("p (b m t) -> p b t m", t=PACK, m=P),
         )
 
-        motif_scale_picked = gather(motif_scale_table[:], motif_list, U8, "motif_scale_picked", WHOLE)
-        motif_scales = keep("motif_scales", [P, S], U8)
-        nc.vector.tensor_copy(motif_scales[:].bitcast(I32), motif_scale_picked[:].bitcast(I32))
-        for a in range(K // PASS):
-            for i in range(2):
-                nc.gpsimd.dma_start(
-                    motif_scales[4 * a + 2 + i : P : 32, :].bitcast(I32),
-                    motif_scale_picked[16 + 4 * a + i : P : 32, :].bitcast(I32),
-                )
-
         w1_mx = {}
         w1_mx[0, 0] = quantise_w1(0, 0)
         w1_mx[1, 0] = quantise_w1(1, 0)
+        w1_mx[0, 1] = quantise_w1(0, 1)
         motif_first = [
             gather(motif_tables[a][:].bitcast(U32), motif_list, U32, "motif_first%d" % a, FIRST) for a in range(K // PASS)
         ]
@@ -179,7 +180,6 @@ def tile_list_wallpaper_repeat_assessor_kernel(
             gather(motif_tables[a][:].bitcast(U32), motif_list, U32, "motif_rest%d" % a, REST) for a in range(K // PASS)
         ]
 
-        w1_mx[0, 1] = quantise_w1(0, 1)
         w1_mx[1, 1] = quantise_w1(1, 1)
 
         w3_raw = [load_rows(w3[b * PASS : (b + 1) * PASS, :], "w3_raw") for b in range(H // PASS)]

@@ -30,6 +30,7 @@ RING = 9
 TURNS_RING = 10
 HALF = CHUNK // 2
 HOLD = 4
+GPSIMD_COLS = 96
 PHASE_BANKS = 6
 TWO_PI = 2.0 * math.pi
 ROUNDER = 1.5 * 2.0**23
@@ -53,8 +54,8 @@ def tile_list_wallpaper_repeat_assessor_kernel(
         page_list = held.tile([P, S // 16], U16, name="page_list")
         amp_cols = keep("amp_cols", [P, H // PASS, PACK], F32)
 
-        def load_rows(rows, name):
-            raw = stage.tile([P, PACK, PASS], F32, name=name, tag="weight_raw", bufs=4)
+        def load_rows(rows, name, slot):
+            raw = stage.tile([P, PACK, PASS], F32, name=name, tag="weight_raw%d" % slot, bufs=1, align_bytes=64)
             nc.sync.dma_start(raw[:], rows.rearrange("(p j) c -> p j c", j=PACK))
             return raw
 
@@ -97,14 +98,14 @@ def tile_list_wallpaper_repeat_assessor_kernel(
 
         nc.sync.dma_start(motif_list[:], offs)
         nc.sync.dma_start(ground_list[:], offs2)
-        w1_raw[0, 0] = load_rows(w1_block(0, 0), "w1_raw")
+        w1_raw[0, 0] = load_rows(w1_block(0, 0), "w1_raw", 0)
         ground_table = load_words(tab2_words[0], "ground_table")
         w2_raw = keep("w2_raw", [P, 2 * H], U8)
         nc.sync.dma_start(w2_raw[:].bitcast(I32), w2_words[0].bitcast(I32))
-        w1_raw[1, 0] = load_rows(w1_block(1, 0), "w1_raw")
-        w1_raw[0, 1] = load_rows(w1_block(0, 1), "w1_raw")
+        w1_raw[1, 0] = load_rows(w1_block(1, 0), "w1_raw", 2)
+        w1_raw[0, 1] = load_rows(w1_block(0, 1), "w1_raw", 1)
         motif_tables = [load_words(tab_words[a], "motif_table%d" % a) for a in range(K // PASS)]
-        w1_raw[1, 1] = load_rows(w1_block(1, 1), "w1_raw")
+        w1_raw[1, 1] = load_rows(w1_block(1, 1), "w1_raw", 3)
         nc.sync.dma_start(amp_cols[:], amp.rearrange("(b p t) -> p b t", p=P, t=PACK))
         style_rows[0, 0] = load_style(0, 0)
         style_rows[0, 1] = load_style(0, 1)
@@ -123,7 +124,7 @@ def tile_list_wallpaper_repeat_assessor_kernel(
             if (a, b) != (1, 1):
                 nc.scalar.activation(dealt, rows, COPY)
             else:
-                nc.gpsimd.tensor_scalar(dealt, rows, 1.0, 0.0, MULT, ADD)
+                nc.vector.tensor_copy(dealt, rows)
             return quantise(grouped, "w1_%d%d" % (a, b))
 
         def quantise_w3(raw, b):
@@ -145,15 +146,6 @@ def tile_list_wallpaper_repeat_assessor_kernel(
 
         FIRST, REST, WHOLE = slice(0, 1), slice(1, CHUNKS), slice(0, CHUNKS)
         motif_scale_picked = gather(motif_scale_table[:], motif_list, U8, "motif_scale_picked", WHOLE)
-        motif_scales = keep("motif_scales", [P, S], U8)
-        nc.vector.tensor_copy(motif_scales[:].bitcast(I32), motif_scale_picked[:].bitcast(I32))
-        for a in range(K // PASS):
-            for i in range(2):
-                nc.scalar.dma_start(
-                    motif_scales[4 * a + 2 + i : P : 32, :].bitcast(I32),
-                    motif_scale_picked[16 + 4 * a + i : P : 32, :].bitcast(I32),
-                )
-
         ground_scales_first = gather(ground_scale_table[:], ground_list, U8, "ground_scales_first", FIRST)
         w2_scale = keep("w2_scale", [P, H], U8)
         nc.gpsimd.tensor_copy(
@@ -170,6 +162,15 @@ def tile_list_wallpaper_repeat_assessor_kernel(
         w1_mx = {}
         w1_mx[0, 0] = quantise_w1(0, 0)
         w1_mx[1, 0] = quantise_w1(1, 0)
+        motif_scales = stage.tile([P, S], U8, name="motif_scales", tag="weight_raw2", bufs=1, align_bytes=64)
+        nc.vector.tensor_copy(motif_scales[:].bitcast(I32), motif_scale_picked[:].bitcast(I32))
+        for a in range(K // PASS):
+            for i in range(2):
+                nc.scalar.dma_start(
+                    motif_scales[4 * a + 2 + i : P : 32, :].bitcast(I32),
+                    motif_scale_picked[16 + 4 * a + i : P : 32, :].bitcast(I32),
+                )
+
         w1_mx[0, 1] = quantise_w1(0, 1)
         motif_first = [
             gather(motif_tables[a][:].bitcast(U32), motif_list, U32, "motif_first%d" % a, FIRST) for a in range(K // PASS)
@@ -182,7 +183,7 @@ def tile_list_wallpaper_repeat_assessor_kernel(
 
         w1_mx[1, 1] = quantise_w1(1, 1)
 
-        w3_raw = [load_rows(w3[b * PASS : (b + 1) * PASS, :], "w3_raw") for b in range(H // PASS)]
+        w3_raw = [load_rows(w3[b * PASS : (b + 1) * PASS, :], "w3_raw", b) for b in range(H // PASS)]
         for b in range(H // PASS):
             style_rows[1, b] = load_style(1, b)
         gain = keep("gain", [P, S], F32)
@@ -229,33 +230,37 @@ def tile_list_wallpaper_repeat_assessor_kernel(
                     stop=(a == K // PASS - 1),
                 )
 
-        def reduce_phases(n, first_product, q, b, h):
+        def count_turns(n, first_product, q, b, h):
             phase = psum.tile([P, 2, CHUNK], F32, name="phase", tag="phase%d" % (n % PHASE_BANKS), bufs=1)
             for e in range(2):
                 first_product(phase[:, e, :], q, b, 2 * h + e)
             shifted = ring(n, [P, 2, CHUNK], U32, "shifted")
             nc.scalar.activation(shifted[:], phase[:], COPY, bias=ROUNDER, scale=1.0 / TWO_PI)
+            return phase, shifted
+
+        def reduce_phases(n, phase, shifted):
             turns = turns_ring(n, [P, 2, CHUNK], F32, "turns")
             nc.scalar.activation(turns[:], shifted[:], COPY, bias=-ROUNDER, scale=1.0)
             reduced = work.tile([P, 2, CHUNK], F32, name="reduced", tag="reduced", bufs=4)
             nc.vector.scalar_tensor_tensor(reduced[:], turns[:], -TWO_PI, phase[:], MULT, ADD)
             return reduced
 
-        def add_style(engine, slot, q, b, e, product):
-            cols = slice(e * HALF, (e + 1) * HALF)
-            z = ring(slot, [P, HALF * PACK], BF16, "z")
-            engine.tensor_tensor(
-                z[:].rearrange("p (c i t) -> p c t i", i=4, t=PACK),
-                product[:, :, cols].rearrange("p t (c i) -> p c t i", i=4),
-                style_rows[q, b][:, :, cols].rearrange("p t (c i) -> p c t i", i=4),
-                ADD,
-            )
+        def add_style(shares, slot, q, b, e, product):
+            z = ring(slot, [P, HALF, PACK], BF16, "z")
+            for engine, first, count in shares:
+                cols = slice(e * HALF + first, e * HALF + first + count)
+                engine.tensor_tensor(
+                    z[:, first : first + count, :].rearrange("p (c i) t -> p c t i", i=4),
+                    product[:, :, cols].rearrange("p t (c i) -> p c t i", i=4),
+                    style_rows[q, b][:, :, cols].rearrange("p t (c i) -> p c t i", i=4),
+                    ADD,
+                )
             return z
 
         def quantise_z(slot, z):
             codes = turns_ring(slot, [P, HALF], U32, "z_codes")
             scales = work.tile([P, HALF], U8, name="z_scales", tag="z_scales", bufs=8, align_bytes=64)
-            nc.vector.quantize_mx(out=codes[:].bitcast(FP8X4), scales=scales[:], in_=z[:])
+            nc.vector.quantize_mx(out=codes[:].bitcast(FP8X4), scales=scales[:], in_=z[:].rearrange("p c t -> p (c t)"))
             return codes, scales
 
         def last_product(q):
@@ -303,24 +308,17 @@ def tile_list_wallpaper_repeat_assessor_kernel(
         to_place = []
         last = len(steps) - 1
         y_late = [work.tile([P, 2 * CHUNK], F32, name="y_late%d" % i) for i in range(2)]
-        for n in range(len(steps) + LAG):
-            if n < len(steps):
-                reduced[n] = reduce_phases(n, *steps[n])
-            if n in to_quantise:
-                key, z = to_quantise[n]
-                z_mx[key] = quantise_z(n, z)
-                if key[1:] == (1, 1):
-                    sums[key[0]] = last_product(key[0])
-                    to_place.extend([(key[0], i) for i in range(N // P)])
-            if n < LAG:
-                continue
-            m = n - LAG
+        counted = {}
+        shared = [(nc.gpsimd, 0, GPSIMD_COLS), (nc.vector, GPSIMD_COLS, HALF - GPSIMD_COLS)]
+        alone = [(nc.vector, 0, HALF)]
+
+        def after_sines(m):
             first_product, q, b, h = steps[m]
-            sines = ring(n, [P, 2, CHUNK], F32, "sines")
+            sines = ring(m + LAG, [P, 2, CHUNK], F32, "sines")
             nc.scalar.activation(sines[:], reduced[m][:], SIN)
             if first_product is ground_product:
-                ground_sines[q, b, h] = (sines, n)
-                continue
+                ground_sines[q, b, h] = (sines, m + LAG)
+                return
             if h == 0:
                 products[q, b] = work.tile([P, PACK, CHUNK], F32, name="product", tag="product", bufs=2)
             ground, ground_slot = ground_sines[q, b, h]
@@ -331,7 +329,7 @@ def tile_list_wallpaper_repeat_assessor_kernel(
                 )
             if to_place and m < last:
                 done, i = to_place.pop(0)
-                y = ring(n, [P, CHUNK], F32, "y")
+                y = turns_ring(m + 1, [P, CHUNK], F32, "y")
                 nc.scalar.copy(y[:], sums[done][i])
                 scatter(i, done, 1, y[:])
             if h == 1:
@@ -340,13 +338,27 @@ def tile_list_wallpaper_repeat_assessor_kernel(
                     w3_mx.append(quantise_w3(w3_raw[b], b))
             if to_add and m < last:
                 key = to_add.pop(0)
-                z = add_style(nc.gpsimd, ground_slot, *key, products[key[:2]])
+                z = add_style(shared, ground_slot, *key, products[key[:2]])
                 to_quantise[min(m + HOLD, last + LAG)] = (key, z)
+
+        for n in range(-1, last + LAG + 2):
+            if n < last:
+                counted[n + 1] = count_turns(n + 1, *steps[n + 1])
+            if n > LAG:
+                after_sines(n - LAG - 1)
+            if 0 <= n <= last:
+                reduced[n] = reduce_phases(n, *counted[n])
+            if n in to_quantise:
+                key, z = to_quantise[n]
+                z_mx[key] = quantise_z(n, z)
+                if key[1:] == (1, 1):
+                    sums[key[0]] = last_product(key[0])
+                    to_place.extend([(key[0], i) for i in range(N // P)])
 
         end = last + LAG
         for k in range(2):
             nc.scalar.copy(y_late[k][:, :CHUNK], sums[CHUNKS - 2][2 + k])
-        z_end = [add_style(nc.vector, end + 1 + k, *key, products[key[:2]]) for k, key in enumerate(to_add)]
+        z_end = [add_style(alone, end + 1 + k, *key, products[key[:2]]) for k, key in enumerate(to_add)]
         for k, key in enumerate(to_add):
             z_mx[key] = quantise_z(end + 1 + k, z_end[k])
         sums_end = last_product(CHUNKS - 1)

@@ -22,16 +22,25 @@ SIN = mybir.ActivationFunctionType.Sin
 P = 128
 PACK = 4
 PASS = P * PACK
+QUADRANTS = 4
+GROUP = 16
+K_PASSES = K // PASS
+R_BLOCKS = H // PASS
+PAGES = N // P
 CHUNK = 256
 CHUNKS = S // CHUNK
-LIST_COLS = CHUNK // 16
-LAG = 2
-RING = 9
-TURNS_RING = 10
+LIST_COLS = CHUNK // GROUP
 HALF = CHUNK // 2
-HOLD = 4
-GPSIMD_COLS = 96
+LINE = 4
+
 PHASE_BANKS = 6
+LAG = 2
+HOLD = 4
+COUNT_BUFFERS = 9
+TURN_BUFFERS = 10
+GPSIMD_COLS = 96
+LATE_PAGES = 2
+
 TWO_PI = 2.0 * math.pi
 ROUNDER = 1.5 * 2.0**23
 
@@ -49,13 +58,13 @@ def tile_list_wallpaper_repeat_assessor_kernel(
         def keep(name, shape, dtype):
             return held.tile(shape, dtype, name=name, align_bytes=64)
 
-        motif_list = held.tile([P, S // 16], U16, name="motif_list")
-        ground_list = held.tile([P, S // 16], U16, name="ground_list")
-        page_list = held.tile([P, S // 16], U16, name="page_list")
-        amp_cols = keep("amp_cols", [P, H // PASS, PACK], F32)
+        motif_list = held.tile([P, S // GROUP], U16, name="motif_list")
+        ground_list = held.tile([P, S // GROUP], U16, name="ground_list")
+        page_list = held.tile([P, S // GROUP], U16, name="page_list")
+        amp_cols = keep("amp_cols", [P, R_BLOCKS, PACK], F32)
 
-        def load_rows(rows, name, slot):
-            raw = stage.tile([P, PACK, PASS], F32, name=name, tag="weight_raw%d" % slot, bufs=1, align_bytes=64)
+        def load_rows(rows, name, buffer):
+            raw = stage.tile([P, PACK, PASS], F32, name=name, tag="weight_raw%d" % buffer, bufs=1, align_bytes=64)
             nc.sync.dma_start(raw[:], rows.rearrange("(p j) c -> p j c", j=PACK))
             return raw
 
@@ -65,7 +74,7 @@ def tile_list_wallpaper_repeat_assessor_kernel(
             return table
 
         def load_style(q, b):
-            rows = stage.tile([P, PACK, CHUNK], F32, name="style_rows", tag="style_rows", bufs=8)
+            rows = stage.tile([P, PACK, CHUNK], F32, name="style_rows", tag="style_rows", bufs=CHUNKS * R_BLOCKS)
             nc.sync.dma_start(
                 rows[:], style[b * PASS : (b + 1) * PASS, q * CHUNK : (q + 1) * CHUNK].rearrange("(p t) j -> p t j", t=PACK)
             )
@@ -74,28 +83,28 @@ def tile_list_wallpaper_repeat_assessor_kernel(
         def w1_block(a, b):
             return w1[a * PASS : (a + 1) * PASS, b * PASS : (b + 1) * PASS]
 
-        w1_raw = {}
-        style_rows = {}
         motif_scale_table = keep("motif_scale_table", [P, T], U8)
         nc.vector.memset(motif_scale_table[:].bitcast(I32), 0)
         ground_scale_table = keep("ground_scale_table", [P, T], U8)
         nc.vector.memset(ground_scale_table[:].bitcast(I32), 0)
         w2_scale_raw = keep("w2_scale_raw", [P, H], U8)
         nc.gpsimd.memset(w2_scale_raw[:].bitcast(I32), 0)
-        for a in range(K // PASS):
+        for a in range(K_PASSES):
             for i in range(2):
                 nc.scalar.dma_start(
-                    motif_scale_table[4 * a + i : P : 16, :].bitcast(I32), tab_scales[a, i:16:2, :].bitcast(I32)
+                    motif_scale_table[4 * a + i : P : GROUP, :].bitcast(I32), tab_scales[a, i:16:2, :].bitcast(I32)
                 )
-        for d in range(4):
+        for d in range(QUADRANTS):
             nc.scalar.dma_start(
                 ground_scale_table[32 * d : 32 * d + 4, :].bitcast(I32), tab2_scales[0, 4 * d : 4 * d + 4, :].bitcast(I32)
             )
-        for d in range(4):
+        for d in range(QUADRANTS):
             nc.gpsimd.dma_start(
                 w2_scale_raw[32 * d : 32 * d + 4, :].bitcast(I32), w2_scales[0, 4 * d : 4 * d + 4, :].bitcast(I32)
             )
 
+        w1_raw = {}
+        style_rows = {}
         nc.sync.dma_start(motif_list[:], offs)
         nc.sync.dma_start(ground_list[:], offs2)
         w1_raw[0, 0] = load_rows(w1_block(0, 0), "w1_raw", 0)
@@ -104,55 +113,67 @@ def tile_list_wallpaper_repeat_assessor_kernel(
         nc.sync.dma_start(w2_raw[:].bitcast(I32), w2_words[0].bitcast(I32))
         w1_raw[1, 0] = load_rows(w1_block(1, 0), "w1_raw", 2)
         w1_raw[0, 1] = load_rows(w1_block(0, 1), "w1_raw", 1)
-        motif_tables = [load_words(tab_words[a], "motif_table%d" % a) for a in range(K // PASS)]
+        motif_tables = [load_words(tab_words[a], "motif_table%d" % a) for a in range(K_PASSES)]
         w1_raw[1, 1] = load_rows(w1_block(1, 1), "w1_raw", 3)
         nc.sync.dma_start(amp_cols[:], amp.rearrange("(b p t) -> p b t", p=P, t=PACK))
-        style_rows[0, 0] = load_style(0, 0)
-        style_rows[0, 1] = load_style(0, 1)
+        for b in range(R_BLOCKS):
+            style_rows[0, b] = load_style(0, b)
 
-        def quantise(grouped, name):
-            width = grouped.shape[1] // PACK
-            codes = keep(name + "_codes", [P, width], U32)
-            scales = keep(name + "_scales", [P, width], U8)
-            nc.vector.quantize_mx(out=codes[:].bitcast(FP8X4), scales=scales[:], in_=grouped[:])
+        def rounded_tile():
+            return stage.tile([P, PACK * PASS], BF16, name="rounded", tag="rounded", bufs=3, align_bytes=64)
+
+        def quantise_weight(rounded, name):
+            codes = keep(name + "_codes", [P, PASS], U32)
+            scales = keep(name + "_scales", [P, PASS], U8)
+            nc.vector.quantize_mx(out=codes[:].bitcast(FP8X4), scales=scales[:], in_=rounded[:])
             return codes, scales
 
-        def quantise_w1(a, b):
-            grouped = stage.tile([P, PACK * PASS], BF16, name="grouped", tag="grouped", bufs=3, align_bytes=64)
-            dealt = grouped[:].rearrange("p (t m j) -> p m t j", t=PACK, j=PACK)
-            rows = w1_raw[a, b][:].rearrange("p j (m t) -> p m t j", t=PACK)
-            if (a, b) != (1, 1):
-                nc.scalar.activation(dealt, rows, COPY)
-            else:
-                nc.vector.tensor_copy(dealt, rows)
-            return quantise(grouped, "w1_%d%d" % (a, b))
+        def round_on_scalar(rounded, raw):
+            nc.scalar.activation(rounded, raw, COPY)
 
-        def quantise_w3(raw, b):
-            grouped = stage.tile([P, PACK * PASS], BF16, name="grouped", tag="grouped", bufs=3, align_bytes=64)
-            nc.vector.tensor_copy(
-                grouped[:].rearrange("p (c i j) -> p c j i", i=4, j=PACK),
-                raw[:].rearrange("p j (c i) -> p c j i", i=4),
+        def quantise_w1(a, b, round_copy):
+            rounded = rounded_tile()
+            round_copy(
+                rounded[:].rearrange("p (t m j) -> p m t j", t=PACK, j=PACK),
+                w1_raw[a, b][:].rearrange("p j (m t) -> p m t j", t=PACK),
             )
-            return quantise(grouped, "w3_%d" % b)
+            return quantise_weight(rounded, "w1_%d%d" % (a, b))
+
+        def quantise_w3(b):
+            rounded = rounded_tile()
+            nc.vector.tensor_copy(
+                rounded[:].rearrange("p (c i j) -> p c j i", i=LINE, j=PACK),
+                w3_raw[b][:].rearrange("p j (c i) -> p c j i", i=LINE),
+            )
+            return quantise_weight(rounded, "w3_%d" % b)
 
         def gather(table, offsets, dtype, name, chunks):
-            width = (chunks.stop - chunks.start) * CHUNK
-            picked = keep(name, [P, width], dtype)
+            picked = keep(name, [P, (chunks.stop - chunks.start) * CHUNK], dtype)
             nc.vector.tensor_copy(picked[:], table.indirect(offsets[:, chunks.start * LIST_COLS : chunks.stop * LIST_COLS]))
             return picked
 
         def chunk_of(first, rest, q):
             return first[:] if q == 0 else rest[:, (q - 1) * CHUNK : q * CHUNK]
 
-        FIRST, REST, WHOLE = slice(0, 1), slice(1, CHUNKS), slice(0, CHUNKS)
-        motif_scale_picked = gather(motif_scale_table[:], motif_list, U8, "motif_scale_picked", WHOLE)
-        ground_scales_first = gather(ground_scale_table[:], ground_list, U8, "ground_scales_first", FIRST)
+        first_chunk, other_chunks, all_chunks = slice(0, 1), slice(1, CHUNKS), slice(0, CHUNKS)
+
+        motif_scale_picked = gather(motif_scale_table[:], motif_list, U8, "motif_scale_picked", all_chunks)
+        motif_scales = keep("motif_scales", [P, S], U8)
+        nc.vector.tensor_copy(motif_scales[:].bitcast(I32), motif_scale_picked[:].bitcast(I32))
+        for a in range(K_PASSES):
+            for i in range(2):
+                nc.scalar.dma_start(
+                    motif_scales[4 * a + 2 + i : P : 32, :].bitcast(I32),
+                    motif_scale_picked[GROUP + 4 * a + i : P : 32, :].bitcast(I32),
+                )
+
+        ground_scales_first = gather(ground_scale_table[:], ground_list, U8, "ground_scales_first", first_chunk)
         w2_scale = keep("w2_scale", [P, H], U8)
         nc.gpsimd.tensor_copy(
             w2_scale[:].rearrange("p (b t m) -> p b t m", t=PACK, m=P),
             w2_scale_raw[:].rearrange("p (b m t) -> p b t m", t=PACK, m=P),
         )
-        ground_first = gather(ground_table[:].bitcast(U32), ground_list, U32, "ground_first", FIRST)
+        ground_first = gather(ground_table[:].bitcast(U32), ground_list, U32, "ground_first", first_chunk)
         w2_codes = keep("w2_codes", [P, 2 * H], U8)
         nc.vector.tensor_copy(
             w2_codes[:].bitcast(U16).rearrange("p (b t m) -> p b t m", t=PACK, m=P),
@@ -160,49 +181,39 @@ def tile_list_wallpaper_repeat_assessor_kernel(
         )
 
         w1_mx = {}
-        w1_mx[0, 0] = quantise_w1(0, 0)
-        w1_mx[1, 0] = quantise_w1(1, 0)
-        motif_scales = stage.tile([P, S], U8, name="motif_scales", tag="weight_raw2", bufs=1, align_bytes=64)
-        nc.vector.tensor_copy(motif_scales[:].bitcast(I32), motif_scale_picked[:].bitcast(I32))
-        for a in range(K // PASS):
-            for i in range(2):
-                nc.scalar.dma_start(
-                    motif_scales[4 * a + 2 + i : P : 32, :].bitcast(I32),
-                    motif_scale_picked[16 + 4 * a + i : P : 32, :].bitcast(I32),
-                )
-
-        w1_mx[0, 1] = quantise_w1(0, 1)
+        w1_mx[0, 0] = quantise_w1(0, 0, round_on_scalar)
+        w1_mx[1, 0] = quantise_w1(1, 0, round_on_scalar)
+        w1_mx[0, 1] = quantise_w1(0, 1, round_on_scalar)
         motif_first = [
-            gather(motif_tables[a][:].bitcast(U32), motif_list, U32, "motif_first%d" % a, FIRST) for a in range(K // PASS)
+            gather(motif_tables[a][:].bitcast(U32), motif_list, U32, "motif_first%d" % a, first_chunk) for a in range(K_PASSES)
         ]
-        ground_scales_rest = gather(ground_scale_table[:], ground_list, U8, "ground_scales_rest", REST)
-        ground_rest = gather(ground_table[:].bitcast(U32), ground_list, U32, "ground_rest", REST)
+        ground_scales_rest = gather(ground_scale_table[:], ground_list, U8, "ground_scales_rest", other_chunks)
+        ground_rest = gather(ground_table[:].bitcast(U32), ground_list, U32, "ground_rest", other_chunks)
         motif_rest = [
-            gather(motif_tables[a][:].bitcast(U32), motif_list, U32, "motif_rest%d" % a, REST) for a in range(K // PASS)
+            gather(motif_tables[a][:].bitcast(U32), motif_list, U32, "motif_rest%d" % a, other_chunks) for a in range(K_PASSES)
         ]
+        w1_mx[1, 1] = quantise_w1(1, 1, nc.vector.tensor_copy)
 
-        w1_mx[1, 1] = quantise_w1(1, 1)
-
-        w3_raw = [load_rows(w3[b * PASS : (b + 1) * PASS, :], "w3_raw", b) for b in range(H // PASS)]
-        for b in range(H // PASS):
+        w3_raw = [load_rows(w3[b * PASS : (b + 1) * PASS, :], "w3_raw", b) for b in range(R_BLOCKS)]
+        for b in range(R_BLOCKS):
             style_rows[1, b] = load_style(1, b)
         gain = keep("gain", [P, S], F32)
         nc.sync.dma_start(gain[:], wgo)
         nc.sync.dma_start(page_list[:], offs3)
         pages = []
-        for i in range(N // P):
+        for i in range(PAGES):
             page = keep("page%d" % i, [P, T], F32)
             nc.sync.dma_start(page[:], page1[i * P : (i + 1) * P, :])
             pages.append(page)
         for q in range(2, CHUNKS):
-            for b in range(H // PASS):
+            for b in range(R_BLOCKS):
                 style_rows[q, b] = load_style(q, b)
 
-        def ring(n, shape, dtype, name):
-            return work.tile(shape, dtype, name=name, tag="ring%d" % (n % RING), bufs=1, align_bytes=64)
+        def count_buffer(n, shape, dtype, name):
+            return work.tile(shape, dtype, name=name, tag="count%d" % (n % COUNT_BUFFERS), bufs=1, align_bytes=64)
 
-        def turns_ring(n, shape, dtype, name):
-            return work.tile(shape, dtype, name=name, tag="turns%d" % (n % TURNS_RING), bufs=1, align_bytes=64)
+        def turn_buffer(n, shape, dtype, name):
+            return work.tile(shape, dtype, name=name, tag="turn%d" % (n % TURN_BUFFERS), bufs=1, align_bytes=64)
 
         def ground_product(phase, q, b, t):
             first = b * PASS + t * P
@@ -218,7 +229,7 @@ def tile_list_wallpaper_repeat_assessor_kernel(
 
         def motif_product(phase, q, b, t):
             cols = slice(t * P, (t + 1) * P)
-            for a in range(K // PASS):
+            for a in range(K_PASSES):
                 codes, scales = w1_mx[a, b]
                 nc.tensor.matmul_mx(
                     out=phase,
@@ -227,147 +238,148 @@ def tile_list_wallpaper_repeat_assessor_kernel(
                     rhs=chunk_of(motif_first[a], motif_rest[a], q).bitcast(FP8X4),
                     rhs_scale=motif_scales[4 * a :, q * CHUNK : (q + 1) * CHUNK],
                     start=(a == 0),
-                    stop=(a == K // PASS - 1),
+                    stop=(a == K_PASSES - 1),
                 )
 
-        def count_turns(n, first_product, q, b, h):
+        def count_turns(n):
+            product, q, b, h = steps[n]
             phase = psum.tile([P, 2, CHUNK], F32, name="phase", tag="phase%d" % (n % PHASE_BANKS), bufs=1)
             for e in range(2):
-                first_product(phase[:, e, :], q, b, 2 * h + e)
-            shifted = ring(n, [P, 2, CHUNK], U32, "shifted")
-            nc.scalar.activation(shifted[:], phase[:], COPY, bias=ROUNDER, scale=1.0 / TWO_PI)
-            return phase, shifted
+                product(phase[:, e, :], q, b, 2 * h + e)
+            counts = count_buffer(n, [P, 2, CHUNK], U32, "counts")
+            nc.scalar.activation(counts[:], phase[:], COPY, bias=ROUNDER, scale=1.0 / TWO_PI)
+            return phase, counts
 
-        def reduce_phases(n, phase, shifted):
-            turns = turns_ring(n, [P, 2, CHUNK], F32, "turns")
-            nc.scalar.activation(turns[:], shifted[:], COPY, bias=-ROUNDER, scale=1.0)
-            reduced = work.tile([P, 2, CHUNK], F32, name="reduced", tag="reduced", bufs=4)
-            nc.vector.scalar_tensor_tensor(reduced[:], turns[:], -TWO_PI, phase[:], MULT, ADD)
-            return reduced
+        def reduce_phases(n, phase, counts):
+            turns = turn_buffer(n, [P, 2, CHUNK], F32, "turns")
+            nc.scalar.activation(turns[:], counts[:], COPY, bias=-ROUNDER, scale=1.0)
+            within = work.tile([P, 2, CHUNK], F32, name="within", tag="within", bufs=LAG + 2)
+            nc.vector.scalar_tensor_tensor(within[:], turns[:], -TWO_PI, phase[:], MULT, ADD)
+            return within
 
-        def add_style(shares, slot, q, b, e, product):
-            z = ring(slot, [P, HALF, PACK], BF16, "z")
-            for engine, first, count in shares:
-                cols = slice(e * HALF + first, e * HALF + first + count)
+        def add_style(shares, buffer, q, b, e):
+            z = count_buffer(buffer, [P, HALF, PACK], BF16, "z")
+            for engine, first, width in shares:
+                cols = slice(e * HALF + first, e * HALF + first + width)
                 engine.tensor_tensor(
-                    z[:, first : first + count, :].rearrange("p (c i) t -> p c t i", i=4),
-                    product[:, :, cols].rearrange("p t (c i) -> p c t i", i=4),
-                    style_rows[q, b][:, :, cols].rearrange("p t (c i) -> p c t i", i=4),
+                    z[:, first : first + width, :].rearrange("p (c i) t -> p c t i", i=LINE),
+                    waves[q, b][:, :, cols].rearrange("p t (c i) -> p c t i", i=LINE),
+                    style_rows[q, b][:, :, cols].rearrange("p t (c i) -> p c t i", i=LINE),
                     ADD,
                 )
             return z
 
-        def quantise_z(slot, z):
-            codes = turns_ring(slot, [P, HALF], U32, "z_codes")
+        def quantise_z(buffer, z):
+            codes = turn_buffer(buffer, [P, HALF], U32, "z_codes")
             scales = work.tile([P, HALF], U8, name="z_scales", tag="z_scales", bufs=8, align_bytes=64)
             nc.vector.quantize_mx(out=codes[:].bitcast(FP8X4), scales=scales[:], in_=z[:].rearrange("p c t -> p (c t)"))
             return codes, scales
 
         def last_product(q):
-            halves = []
-            for pair in range(N // P // 2):
-                sums = psum.tile([P, 2, CHUNK], F32, name="sums", tag="sums%d" % pair, bufs=1)
-                for half in range(2):
-                    cols = slice((2 * pair + half) * P, (2 * pair + half + 1) * P)
+            by_page = []
+            for bank in range(PAGES // 2):
+                sums = psum.tile([P, 2, CHUNK], F32, name="sums", tag="sums%d" % bank, bufs=1)
+                for side in range(2):
+                    cols = slice((2 * bank + side) * P, (2 * bank + side + 1) * P)
                     for e in range(2):
-                        for b in range(H // PASS):
+                        for b in range(R_BLOCKS):
                             nc.tensor.matmul_mx(
-                                out=sums[:, half, e * HALF : (e + 1) * HALF],
+                                out=sums[:, side, e * HALF : (e + 1) * HALF],
                                 lhsT=w3_mx[b][0][:, cols].bitcast(FP8X4),
                                 lhsT_scale=w3_mx[b][1][:, cols],
                                 rhs=z_mx[q, b, e][0][:].bitcast(FP8X4),
                                 rhs_scale=z_mx[q, b, e][1][:],
                                 start=(b == 0),
-                                stop=(b == H // PASS - 1),
+                                stop=(b == R_BLOCKS - 1),
                             )
-                    halves.append(sums[:, half, :])
-            return halves
+                    by_page.append(sums[:, side, :])
+            return by_page
 
-        def scatter(i, first_chunk, chunks, y):
+        def scatter(i, q, chunks, y):
             nc.vector.tensor_tensor(
-                pages[i][:].indirect(page_list[:, first_chunk * LIST_COLS : (first_chunk + chunks) * LIST_COLS]),
+                pages[i][:].indirect(page_list[:, q * LIST_COLS : (q + chunks) * LIST_COLS]),
                 y,
-                gain[:, first_chunk * CHUNK : (first_chunk + chunks) * CHUNK],
+                gain[:, q * CHUNK : (q + chunks) * CHUNK],
                 MULT,
             )
 
-        pairs = [(b, h) for b in range(H // PASS) for h in range(PACK // 2)]
+        pairs = [(b, h) for b in range(R_BLOCKS) for h in range(PACK // 2)]
         steps = [(ground_product, 0, b, h) for b, h in pairs] + [(motif_product, 0, b, h) for b, h in pairs]
         for q in range(1, CHUNKS):
             for b, h in pairs:
                 steps.extend([(ground_product, q, b, h), (motif_product, q, b, h)])
+        last = len(steps) - 1
 
-        w3_mx = []
+        counted = {}
         reduced = {}
         ground_sines = {}
+        waves = {}
         z_mx = {}
-        sums = {}
-        products = {}
+        w3_mx = []
+        y_sums = {}
         to_add = []
         to_quantise = {}
         to_place = []
-        last = len(steps) - 1
-        y_late = [work.tile([P, 2 * CHUNK], F32, name="y_late%d" % i) for i in range(2)]
-        counted = {}
+        y_late = [work.tile([P, 2 * CHUNK], F32, name="y_late%d" % k) for k in range(LATE_PAGES)]
         shared = [(nc.gpsimd, 0, GPSIMD_COLS), (nc.vector, GPSIMD_COLS, HALF - GPSIMD_COLS)]
-        alone = [(nc.vector, 0, HALF)]
+        vector_alone = [(nc.vector, 0, HALF)]
 
-        def after_sines(m):
-            first_product, q, b, h = steps[m]
-            sines = ring(m + LAG, [P, 2, CHUNK], F32, "sines")
+        def take_sines(m):
+            product, q, b, h = steps[m]
+            sines = count_buffer(m + LAG, [P, 2, CHUNK], F32, "sines")
             nc.scalar.activation(sines[:], reduced[m][:], SIN)
-            if first_product is ground_product:
+            if product is ground_product:
                 ground_sines[q, b, h] = (sines, m + LAG)
                 return
             if h == 0:
-                products[q, b] = work.tile([P, PACK, CHUNK], F32, name="product", tag="product", bufs=2)
-            ground, ground_slot = ground_sines[q, b, h]
+                waves[q, b] = work.tile([P, PACK, CHUNK], F32, name="waves", tag="waves", bufs=2)
+            ground, ground_buffer = ground_sines[q, b, h]
             for e in range(2):
                 t = 2 * h + e
                 nc.vector.scalar_tensor_tensor(
-                    products[q, b][:, t, :], sines[:, e, :], amp_cols[:, b, t : t + 1], ground[:, e, :], MULT, MULT
+                    waves[q, b][:, t, :], sines[:, e, :], amp_cols[:, b, t : t + 1], ground[:, e, :], MULT, MULT
                 )
             if to_place and m < last:
                 done, i = to_place.pop(0)
-                y = turns_ring(m + 1, [P, CHUNK], F32, "y")
-                nc.scalar.copy(y[:], sums[done][i])
+                y = turn_buffer(m + 1, [P, CHUNK], F32, "y")
+                nc.scalar.copy(y[:], y_sums[done][i])
                 scatter(i, done, 1, y[:])
             if h == 1:
                 to_add.extend([(q, b, 0), (q, b, 1)])
                 if q == 0:
-                    w3_mx.append(quantise_w3(w3_raw[b], b))
+                    w3_mx.append(quantise_w3(b))
             if to_add and m < last:
-                key = to_add.pop(0)
-                z = add_style(shared, ground_slot, *key, products[key[:2]])
-                to_quantise[min(m + HOLD, last + LAG)] = (key, z)
+                half = to_add.pop(0)
+                to_quantise[min(m + HOLD, last + LAG)] = (half, add_style(shared, ground_buffer, *half))
 
         for n in range(-1, last + LAG + 2):
             if n < last:
-                counted[n + 1] = count_turns(n + 1, *steps[n + 1])
+                counted[n + 1] = count_turns(n + 1)
             if n > LAG:
-                after_sines(n - LAG - 1)
+                take_sines(n - LAG - 1)
             if 0 <= n <= last:
                 reduced[n] = reduce_phases(n, *counted[n])
             if n in to_quantise:
-                key, z = to_quantise[n]
-                z_mx[key] = quantise_z(n, z)
-                if key[1:] == (1, 1):
-                    sums[key[0]] = last_product(key[0])
-                    to_place.extend([(key[0], i) for i in range(N // P)])
+                half, z = to_quantise[n]
+                z_mx[half] = quantise_z(n, z)
+                if half[1:] == (R_BLOCKS - 1, 1):
+                    y_sums[half[0]] = last_product(half[0])
+                    to_place.extend([(half[0], i) for i in range(PAGES)])
 
-        end = last + LAG
-        for k in range(2):
-            nc.scalar.copy(y_late[k][:, :CHUNK], sums[CHUNKS - 2][2 + k])
-        z_end = [add_style(alone, end + 1 + k, *key, products[key[:2]]) for k, key in enumerate(to_add)]
-        for k, key in enumerate(to_add):
-            z_mx[key] = quantise_z(end + 1 + k, z_end[k])
-        sums_end = last_product(CHUNKS - 1)
-        for i in range(2):
-            y = work.tile([P, CHUNK], F32, name="y_end", tag="y_end", bufs=2)
-            nc.scalar.copy(y[:], sums_end[i])
+        early_pages = PAGES - LATE_PAGES
+        spare = last + LAG + 1
+        for k in range(LATE_PAGES):
+            nc.scalar.copy(y_late[k][:, :CHUNK], y_sums[CHUNKS - 2][early_pages + k])
+        z_end = [add_style(vector_alone, spare + k, *half) for k, half in enumerate(to_add)]
+        for k, half in enumerate(to_add):
+            z_mx[half] = quantise_z(spare + k, z_end[k])
+        y_sums[CHUNKS - 1] = last_product(CHUNKS - 1)
+        for i in range(early_pages):
+            y = work.tile([P, CHUNK], F32, name="y_end", tag="y_end", bufs=early_pages)
+            nc.scalar.copy(y[:], y_sums[CHUNKS - 1][i])
             scatter(i, CHUNKS - 1, 1, y[:])
-        for k in range(2):
-            nc.scalar.copy(y_late[k][:, CHUNK:], sums_end[2 + k])
-            scatter(2 + k, CHUNKS - 2, 2, y_late[k][:])
-        for i in range(N // P):
+        for k in range(LATE_PAGES):
+            nc.scalar.copy(y_late[k][:, CHUNK:], y_sums[CHUNKS - 1][early_pages + k])
+            scatter(early_pages + k, CHUNKS - 2, 2, y_late[k][:])
+        for i in range(PAGES):
             nc.sync.dma_start(out[i * P : (i + 1) * P, :], pages[i][:])

import math
from contextlib import ExitStack

import concourse.mybir as mybir

S, T, K, K2, H, N = 1024, 2048, 1024, 512, 1024, 512
FLOPS = 2 * S * (K * H + K2 * H + H * N)

F32 = mybir.dt.float32
BF16 = mybir.dt.bfloat16
I32 = mybir.dt.int32
U32 = mybir.dt.uint32
U16 = mybir.dt.uint16
U8 = mybir.dt.uint8
FP8X4 = mybir.dt.float8_e4m3fn_x4
FP4X4 = mybir.dt.float4_e2m1fn_x4
MULT = mybir.AluOpType.mult
ADD = mybir.AluOpType.add
COPY = mybir.ActivationFunctionType.Copy
SIN = mybir.ActivationFunctionType.Sin

P = 128
PACK = 4
PASS = P * PACK
QUADRANTS = 4
GROUP = 16
K_PASSES = K // PASS
R_BLOCKS = H // PASS
PAGES = N // P
CHUNK = 256
CHUNKS = S // CHUNK
LIST_COLS = CHUNK // GROUP
HALF = CHUNK // 2
LINE = 4

PHASE_BANKS = 6
LAG = 2
HOLD = 4
COUNT_BUFFERS = 9
TURN_BUFFERS = 10
GPSIMD_COLS = 96
LATE_PAGES = 2

TWO_PI = 2.0 * math.pi
ROUNDER = 1.5 * 2.0**23


def tile_list_wallpaper_repeat_assessor_kernel(
    tc, tab_words, tab_scales, offs, tab2_words, tab2_scales, offs2, offs3, w1, w2_words, w2_scales, amp, style, w3, wgo, page1, out
):
    nc = tc.nc
    with ExitStack() as ctx:
        held = ctx.enter_context(tc.tile_pool(name="held", bufs=1))
        stage = ctx.enter_context(tc.tile_pool(name="stage", bufs=1))
        work = ctx.enter_context(tc.tile_pool(name="work", bufs=1))
        psum = ctx.enter_context(tc.psum_pool(name="psum", bufs=1))

        def keep(name, shape, dtype):
            return held.tile(shape, dtype, name=name, align_bytes=64)

        motif_list = held.tile([P, S // GROUP], U16, name="motif_list")
        ground_list = held.tile([P, S // GROUP], U16, name="ground_list")
        page_list = held.tile([P, S // GROUP], U16, name="page_list")
        amp_cols = keep("amp_cols", [P, R_BLOCKS, PACK], F32)

        def load_rows(rows, name, buffer):
            raw = stage.tile([P, PACK, PASS], F32, name=name, tag="weight_raw%d" % buffer, bufs=1, align_bytes=64)
            nc.sync.dma_start(raw[:], rows.rearrange("(p j) c -> p j c", j=PACK))
            return raw

        def load_words(words, name):
            table = keep(name, [P, T], I32)
            nc.sync.dma_start(table[:], words.rearrange("p t i -> p (t i)").bitcast(I32))
            return table

        def load_style(q, b):
            rows = stage.tile([P, PACK, CHUNK], F32, name="style_rows", tag="style_rows", bufs=CHUNKS * R_BLOCKS)
            nc.sync.dma_start(
                rows[:], style[b * PASS : (b + 1) * PASS, q * CHUNK : (q + 1) * CHUNK].rearrange("(p t) j -> p t j", t=PACK)
            )
            return rows

        def w1_block(a, b):
            return w1[a * PASS : (a + 1) * PASS, b * PASS : (b + 1) * PASS]

        motif_scale_table = keep("motif_scale_table", [P, T], U8)
        nc.vector.memset(motif_scale_table[:].bitcast(I32), 0)
        ground_scale_table = keep("ground_scale_table", [P, T], U8)
        nc.vector.memset(ground_scale_table[:].bitcast(I32), 0)
        w2_scale_raw = keep("w2_scale_raw", [P, H], U8)
        nc.gpsimd.memset(w2_scale_raw[:].bitcast(I32), 0)
        for a in range(K_PASSES):
            for i in range(2):
                nc.scalar.dma_start(
                    motif_scale_table[4 * a + i : P : GROUP, :].bitcast(I32), tab_scales[a, i:16:2, :].bitcast(I32)
                )
        for d in range(QUADRANTS):
            nc.scalar.dma_start(
                ground_scale_table[32 * d : 32 * d + 4, :].bitcast(I32), tab2_scales[0, 4 * d : 4 * d + 4, :].bitcast(I32)
            )
        for d in range(QUADRANTS):
            nc.gpsimd.dma_start(
                w2_scale_raw[32 * d : 32 * d + 4, :].bitcast(I32), w2_scales[0, 4 * d : 4 * d + 4, :].bitcast(I32)
            )

        w1_raw = {}
        style_rows = {}
        nc.sync.dma_start(motif_list[:], offs)
        nc.sync.dma_start(ground_list[:], offs2)
        w1_raw[0, 0] = load_rows(w1_block(0, 0), "w1_raw", 0)
        ground_table = load_words(tab2_words[0], "ground_table")
        w2_raw = keep("w2_raw", [P, 2 * H], U8)
        nc.sync.dma_start(w2_raw[:].bitcast(I32), w2_words[0].bitcast(I32))
        w1_raw[1, 0] = load_rows(w1_block(1, 0), "w1_raw", 2)
        w1_raw[0, 1] = load_rows(w1_block(0, 1), "w1_raw", 1)
        motif_tables = [load_words(tab_words[a], "motif_table%d" % a) for a in range(K_PASSES)]
        w1_raw[1, 1] = load_rows(w1_block(1, 1), "w1_raw", 3)
        nc.sync.dma_start(amp_cols[:], amp.rearrange("(b p t) -> p b t", p=P, t=PACK))
        for b in range(R_BLOCKS):
            style_rows[0, b] = load_style(0, b)

        def rounded_tile():
            return stage.tile([P, PACK * PASS], BF16, name="rounded", tag="rounded", bufs=3, align_bytes=64)

        def quantise_weight(rounded, name):
            codes = keep(name + "_codes", [P, PASS], U32)
            scales = keep(name + "_scales", [P, PASS], U8)
            nc.vector.quantize_mx(out=codes[:].bitcast(FP8X4), scales=scales[:], in_=rounded[:])
            return codes, scales

        def round_on_scalar(rounded, raw):
            nc.scalar.activation(rounded, raw, COPY)

        def quantise_w1(a, b, round_copy):
            rounded = rounded_tile()
            round_copy(
                rounded[:].rearrange("p (t m j) -> p m t j", t=PACK, j=PACK),
                w1_raw[a, b][:].rearrange("p j (m t) -> p m t j", t=PACK),
            )
            return quantise_weight(rounded, "w1_%d%d" % (a, b))

        def quantise_w3(b):
            rounded = rounded_tile()
            nc.vector.tensor_copy(
                rounded[:].rearrange("p (c i j) -> p c j i", i=LINE, j=PACK),
                w3_raw[b][:].rearrange("p j (c i) -> p c j i", i=LINE),
            )
            return quantise_weight(rounded, "w3_%d" % b)

        def gather(table, offsets, dtype, name, chunks):
            picked = keep(name, [P, (chunks.stop - chunks.start) * CHUNK], dtype)
            nc.vector.tensor_copy(picked[:], table.indirect(offsets[:, chunks.start * LIST_COLS : chunks.stop * LIST_COLS]))
            return picked

        def chunk_of(first, rest, q):
            return first[:] if q == 0 else rest[:, (q - 1) * CHUNK : q * CHUNK]

        first_chunk, other_chunks, all_chunks = slice(0, 1), slice(1, CHUNKS), slice(0, CHUNKS)

        motif_scale_picked = gather(motif_scale_table[:], motif_list, U8, "motif_scale_picked", all_chunks)
        motif_scales = keep("motif_scales", [P, S], U8)
        nc.vector.tensor_copy(motif_scales[:].bitcast(I32), motif_scale_picked[:].bitcast(I32))
        for a in range(K_PASSES):
            for i in range(2):
                nc.scalar.dma_start(
                    motif_scales[4 * a + 2 + i : P : 32, :].bitcast(I32),
                    motif_scale_picked[GROUP + 4 * a + i : P : 32, :].bitcast(I32),
                )

        ground_scales_first = gather(ground_scale_table[:], ground_list, U8, "ground_scales_first", first_chunk)
        w2_scale = keep("w2_scale", [P, H], U8)
        nc.gpsimd.tensor_copy(
            w2_scale[:].rearrange("p (b t m) -> p b t m", t=PACK, m=P),
            w2_scale_raw[:].rearrange("p (b m t) -> p b t m", t=PACK, m=P),
        )
        ground_first = gather(ground_table[:].bitcast(U32), ground_list, U32, "ground_first", first_chunk)
        w2_codes = keep("w2_codes", [P, 2 * H], U8)
        nc.vector.tensor_copy(
            w2_codes[:].bitcast(U16).rearrange("p (b t m) -> p b t m", t=PACK, m=P),
            w2_raw[:].bitcast(U16).rearrange("p (b m t) -> p b t m", t=PACK, m=P),
        )

        w1_mx = {}
        w1_mx[0, 0] = quantise_w1(0, 0, round_on_scalar)
        w1_mx[1, 0] = quantise_w1(1, 0, round_on_scalar)
        w1_mx[0, 1] = quantise_w1(0, 1, round_on_scalar)
        motif_first = [
            gather(motif_tables[a][:].bitcast(U32), motif_list, U32, "motif_first%d" % a, first_chunk) for a in range(K_PASSES)
        ]
        ground_scales_rest = gather(ground_scale_table[:], ground_list, U8, "ground_scales_rest", other_chunks)
        ground_rest = gather(ground_table[:].bitcast(U32), ground_list, U32, "ground_rest", other_chunks)
        motif_rest = [
            gather(motif_tables[a][:].bitcast(U32), motif_list, U32, "motif_rest%d" % a, other_chunks) for a in range(K_PASSES)
        ]
        w1_mx[1, 1] = quantise_w1(1, 1, nc.vector.tensor_copy)

        w3_raw = [load_rows(w3[b * PASS : (b + 1) * PASS, :], "w3_raw", b) for b in range(R_BLOCKS)]
        for b in range(R_BLOCKS):
            style_rows[1, b] = load_style(1, b)
        gain = keep("gain", [P, S], F32)
        nc.sync.dma_start(gain[:], wgo)
        nc.sync.dma_start(page_list[:], offs3)
        pages = []
        for i in range(PAGES):
            page = keep("page%d" % i, [P, T], F32)
            nc.sync.dma_start(page[:], page1[i * P : (i + 1) * P, :])
            pages.append(page)
        for q in range(2, CHUNKS):
            for b in range(R_BLOCKS):
                style_rows[q, b] = load_style(q, b)

        def count_buffer(n, shape, dtype, name):
            return work.tile(shape, dtype, name=name, tag="count%d" % (n % COUNT_BUFFERS), bufs=1, align_bytes=64)

        def turn_buffer(n, shape, dtype, name):
            return work.tile(shape, dtype, name=name, tag="turn%d" % (n % TURN_BUFFERS), bufs=1, align_bytes=64)

        def ground_product(phase, q, b, t):
            first = b * PASS + t * P
            nc.tensor.matmul_mx(
                out=phase,
                lhsT=w2_codes[:, 2 * first : 2 * (first + P)].bitcast(FP4X4),
                lhsT_scale=w2_scale[:, first : first + P],
                rhs=chunk_of(ground_first, ground_rest, q).bitcast(FP8X4),
                rhs_scale=chunk_of(ground_scales_first, ground_scales_rest, q),
                start=True,
                stop=True,
            )

        def motif_product(phase, q, b, t):
            cols = slice(t * P, (t + 1) * P)
            for a in range(K_PASSES):
                codes, scales = w1_mx[a, b]
                nc.tensor.matmul_mx(
                    out=phase,
                    lhsT=codes[:, cols].bitcast(FP8X4),
                    lhsT_scale=scales[:, cols],
                    rhs=chunk_of(motif_first[a], motif_rest[a], q).bitcast(FP8X4),
                    rhs_scale=motif_scales[4 * a :, q * CHUNK : (q + 1) * CHUNK],
                    start=(a == 0),
                    stop=(a == K_PASSES - 1),
                )

        def count_turns(n):
            product, q, b, h = steps[n]
            phase = psum.tile([P, 2, CHUNK], F32, name="phase", tag="phase%d" % (n % PHASE_BANKS), bufs=1)
            for e in range(2):
                product(phase[:, e, :], q, b, 2 * h + e)
            counts = count_buffer(n, [P, 2, CHUNK], U32, "counts")
            nc.scalar.activation(counts[:], phase[:], COPY, bias=ROUNDER, scale=1.0 / TWO_PI)
            return phase, counts

        def reduce_phases(n, phase, counts):
            turns = turn_buffer(n, [P, 2, CHUNK], F32, "turns")
            nc.scalar.activation(turns[:], counts[:], COPY, bias=-ROUNDER, scale=1.0)
            within = work.tile([P, 2, CHUNK], F32, name="within", tag="within", bufs=LAG + 2)
            nc.vector.scalar_tensor_tensor(within[:], turns[:], -TWO_PI, phase[:], MULT, ADD)
            return within

        def add_style(shares, buffer, q, b, e):
            z = count_buffer(buffer, [P, HALF, PACK], BF16, "z")
            for engine, first, width in shares:
                cols = slice(e * HALF + first, e * HALF + first + width)
                engine.tensor_tensor(
                    z[:, first : first + width, :].rearrange("p (c i) t -> p c t i", i=LINE),
                    waves[q, b][:, :, cols].rearrange("p t (c i) -> p c t i", i=LINE),
                    style_rows[q, b][:, :, cols].rearrange("p t (c i) -> p c t i", i=LINE),
                    ADD,
                )
            return z

        def quantise_z(buffer, z):
            codes = turn_buffer(buffer, [P, HALF], U32, "z_codes")
            scales = work.tile([P, HALF], U8, name="z_scales", tag="z_scales", bufs=8, align_bytes=64)
            nc.vector.quantize_mx(out=codes[:].bitcast(FP8X4), scales=scales[:], in_=z[:].rearrange("p c t -> p (c t)"))
            return codes, scales

        def last_product(q):
            by_page = []
            for bank in range(PAGES // 2):
                sums = psum.tile([P, 2, CHUNK], F32, name="sums", tag="sums%d" % bank, bufs=1)
                for side in range(2):
                    cols = slice((2 * bank + side) * P, (2 * bank + side + 1) * P)
                    for e in range(2):
                        for b in range(R_BLOCKS):
                            nc.tensor.matmul_mx(
                                out=sums[:, side, e * HALF : (e + 1) * HALF],
                                lhsT=w3_mx[b][0][:, cols].bitcast(FP8X4),
                                lhsT_scale=w3_mx[b][1][:, cols],
                                rhs=z_mx[q, b, e][0][:].bitcast(FP8X4),
                                rhs_scale=z_mx[q, b, e][1][:],
                                start=(b == 0),
                                stop=(b == R_BLOCKS - 1),
                            )
                    by_page.append(sums[:, side, :])
            return by_page

        def scatter(i, q, chunks, y):
            nc.vector.tensor_tensor(
                pages[i][:].indirect(page_list[:, q * LIST_COLS : (q + chunks) * LIST_COLS]),
                y,
                gain[:, q * CHUNK : (q + chunks) * CHUNK],
                MULT,
            )

        pairs = [(b, h) for b in range(R_BLOCKS) for h in range(PACK // 2)]
        steps = [(ground_product, 0, b, h) for b, h in pairs] + [(motif_product, 0, b, h) for b, h in pairs]
        for q in range(1, CHUNKS):
            for b, h in pairs:
                steps.extend([(ground_product, q, b, h), (motif_product, q, b, h)])
        last = len(steps) - 1

        counted = {}
        reduced = {}
        ground_sines = {}
        waves = {}
        z_mx = {}
        w3_mx = []
        y_sums = {}
        to_add = []
        to_quantise = {}
        to_place = []
        y_late = [work.tile([P, 2 * CHUNK], F32, name="y_late%d" % k) for k in range(LATE_PAGES)]
        shared = [(nc.gpsimd, 0, GPSIMD_COLS), (nc.vector, GPSIMD_COLS, HALF - GPSIMD_COLS)]
        vector_alone = [(nc.vector, 0, HALF)]

        def take_sines(m):
            product, q, b, h = steps[m]
            sines = count_buffer(m + LAG, [P, 2, CHUNK], F32, "sines")
            nc.scalar.activation(sines[:], reduced[m][:], SIN)
            if product is ground_product:
                ground_sines[q, b, h] = (sines, m + LAG)
                return
            if h == 0:
                waves[q, b] = work.tile([P, PACK, CHUNK], F32, name="waves", tag="waves", bufs=2)
            ground, ground_buffer = ground_sines[q, b, h]
            for e in range(2):
                t = 2 * h + e
                nc.vector.scalar_tensor_tensor(
                    waves[q, b][:, t, :], sines[:, e, :], amp_cols[:, b, t : t + 1], ground[:, e, :], MULT, MULT
                )
            if to_place and m < last:
                done, i = to_place.pop(0)
                y = turn_buffer(m + 1, [P, CHUNK], F32, "y")
                nc.scalar.copy(y[:], y_sums[done][i])
                scatter(i, done, 1, y[:])
            if h == 1:
                to_add.extend([(q, b, 0), (q, b, 1)])
                if q == 0:
                    w3_mx.append(quantise_w3(b))
            if to_add and m < last:
                half = to_add.pop(0)
                to_quantise[min(m + HOLD, last + LAG)] = (half, add_style(shared, ground_buffer, *half))

        for n in range(-1, last + LAG + 2):
            if n < last:
                counted[n + 1] = count_turns(n + 1)
            if n > LAG:
                take_sines(n - LAG - 1)
            if 0 <= n <= last:
                reduced[n] = reduce_phases(n, *counted[n])
            if n in to_quantise:
                half, z = to_quantise[n]
                z_mx[half] = quantise_z(n, z)
                if half[1:] == (R_BLOCKS - 1, 1):
                    y_sums[half[0]] = last_product(half[0])
                    to_place.extend([(half[0], i) for i in range(PAGES)])

        early_pages = PAGES - LATE_PAGES
        spare = last + LAG + 1
        for k in range(LATE_PAGES):
            nc.scalar.copy(y_late[k][:, :CHUNK], y_sums[CHUNKS - 2][early_pages + k])
        z_end = [add_style(vector_alone, spare + k, *half) for k, half in enumerate(to_add)]
        for k, half in enumerate(to_add):
            z_mx[half] = quantise_z(spare + k, z_end[k])
        y_sums[CHUNKS - 1] = last_product(CHUNKS - 1)
        for i in range(early_pages):
            y = work.tile([P, CHUNK], F32, name="y_end", tag="y_end", bufs=early_pages)
            nc.scalar.copy(y[:], y_sums[CHUNKS - 1][i])
            scatter(i, CHUNKS - 1, 1, y[:])
        for k in range(LATE_PAGES):
            nc.scalar.copy(y_late[k][:, CHUNK:], y_sums[CHUNKS - 1][early_pages + k])
            scatter(early_pages + k, CHUNKS - 2, 2, y_late[k][:])
        for i in range(PAGES):
            nc.sync.dma_start(out[i * P : (i + 1) * P, :], pages[i][:])
